import numpy as np
import ml_dtypes


def mxq(x, axis, fmt="e4m3"):
    dtype, down = {"e4m3": (ml_dtypes.float8_e4m3fn, 7), "e5m2": (ml_dtypes.float8_e5m2, 14)}[fmt]
    v = np.moveaxis(np.asarray(x, np.float32).astype(ml_dtypes.bfloat16).astype(np.float64), axis, -1)
    blocks = v.reshape(v.shape[:-1] + (-1, 32))
    amax = np.abs(blocks).max(-1, keepdims=True)
    byte = np.maximum(np.where(amax > 0, np.frexp(amax)[1] - 1 + 127, 0) - down, 1)
    scale = np.exp2(byte - 127.0)
    codes = (blocks / scale).astype(np.float32).astype(dtype).astype(np.float64)
    return np.moveaxis((codes * scale).reshape(v.shape), -1, axis)


WIDE = False


def mx_kscale(k):
    if not WIDE:
        return np.ones(k)
    levels = np.array([10, -10, 5, -5, 0])
    if k % 512:
        return np.exp2(np.random.permutation(np.resize(levels, k // 32))).repeat(32)
    a = np.empty((k // 512, 16))
    for p in range(k // 512):
        a[p, :8] = np.random.permutation(np.resize(levels, 8))
        for g in range(8):
            far = levels[np.abs(levels - a[p, g]) >= 10]
            a[p, g + 8] = far[np.random.randint(len(far))]
    return np.exp2(a.ravel()).repeat(32)


def f64(x):
    return np.asarray(x).astype(np.float64)


def striped(idx):
    return np.tile(idx.reshape(-1, 16).T, (8, 1)).astype(np.uint16)


def unstriped(offs):
    return offs[:16].T.reshape(-1).astype(np.int64)


def pack_weight(w):
    k, n = w.shape
    w = f64(np.asarray(w, np.float32).astype(ml_dtypes.bfloat16)).reshape(k // 32, 32, n)
    amax = np.abs(w).max(1)
    byte = np.clip(np.where(amax > 0, np.frexp(amax)[1] - 1 + 127 - 7, 1), 1, 254)
    scaled = (w * np.exp2(127.0 - byte)[:, None, :]).reshape(k, n).astype(np.float32)
    words = np.ascontiguousarray(scaled.reshape(k // 512, 128, 4, n).transpose(0, 1, 3, 2)).astype(ml_dtypes.float8_e4m3fn).view(np.uint8)
    return words, np.ascontiguousarray(byte.astype(np.uint8).reshape(k // 512, 16, n))


def unpack_weight(words, scales):
    g, p, n, _ = words.shape
    vals = np.ascontiguousarray(words).view(ml_dtypes.float8_e4m3fn).astype(np.float64) * np.repeat(np.exp2(scales.astype(np.float64) - 127.0), 8, axis=1)[..., None]
    return vals.transpose(0, 1, 3, 2).reshape(g * 512, n)


K, T, S, N, U = 512, 2048, 1024, 256, 1024


def setup_inputs():
    n = np.random.standard_normal
    s = mx_kscale(K)[:, None]
    packed_xT = pack_weight(n((K, T)) * s)
    return {
        "x_words": packed_xT[0],
        "x_scales": packed_xT[1],
        "w1": (n((K, N)) / np.sqrt(K) / s).astype(np.float32),
        "scale": np.random.uniform(0.5, 1.5, (N, U)).astype(np.float32),
        "offs": striped(np.random.permutation(T)[:S]),
        "task": striped(np.random.permutation(U)[(U * np.random.uniform(0, 1, S) ** 4).astype(np.int64)]),
    }


def reference(x_words, x_scales, w1, scale, offs, task):
    xq = unpack_weight(x_words, x_scales)[:, unstriped(offs)]
    y = mxq(f64(w1), 0, "e4m3").T @ xq
    g = f64(scale)[:, unstriped(task)]
    return y * g

@@ -1,0 +1,79 @@
+from contextlib import ExitStack
+
+import concourse.mybir as mybir
+
+K, T, S, N, U = 512, 2048, 1024, 256, 1024
+FLOPS = 2 * K * N * S
+
+F32 = mybir.dt.float32
+BF16 = mybir.dt.bfloat16
+I32 = mybir.dt.int32
+U32 = mybir.dt.uint32
+U16 = mybir.dt.uint16
+U8 = mybir.dt.uint8
+FP8X4 = mybir.dt.float8_e4m3fn_x4
+MULT = mybir.AluOpType.mult
+
+P = 128
+PACK = 4
+LIST = 16
+HALF = 512
+
+
+def tile_picked_none_p_kernel(tc, x_words, x_scales, w1, scale, offs, task, out):
+    nc = tc.nc
+    with ExitStack() as ctx:
+        lists = ctx.enter_context(tc.tile_pool(name="lists", bufs=1))
+        keep = ctx.enter_context(tc.tile_pool(name="keep", bufs=1))
+        psum = ctx.enter_context(tc.psum_pool(name="psum", bufs=1))
+
+        offs_sb = lists.tile([P, S // LIST], U16, name="offs_sb")
+        task_sb = lists.tile([P, S // LIST], U16, name="task_sb")
+        byte_table = keep.tile([P, T], U8, name="byte_table", align_bytes=64)
+        word_table = keep.tile([P, T], U32, name="word_table", align_bytes=64)
+        w_raw = keep.tile([P, PACK, N], F32, name="w_raw", align_bytes=64)
+        tables = [keep.tile([P, U], F32, name=f"scale_table{m}", align_bytes=64) for m in range(N // P)]
+
+        nc.vector.memset(byte_table[:].bitcast(I32), 0)
+        nc.sync.dma_start(offs_sb[:], offs)
+        for q in range(4):
+            nc.scalar.dma_start(byte_table[32 * q : 32 * q + 4, :].bitcast(I32), x_scales[0, 4 * q : 4 * q + 4, :].bitcast(I32))
+        nc.sync.dma_start(w_raw[:], w1.rearrange("(p j) n -> p j n", j=PACK))
+        nc.sync.dma_start(word_table[:].bitcast(I32), x_words[0].rearrange("p t r -> p (t r)").bitcast(I32))
+        nc.sync.dma_start(task_sb[:], task)
+        for m in range(N // P):
+            nc.sync.dma_start(tables[m][:], scale[m * P : (m + 1) * P, :])
+
+        w_grouped = keep.tile([P, N, PACK], BF16, name="w_grouped", align_bytes=64)
+        nc.scalar.copy(w_grouped[:], w_raw[:].rearrange("p j n -> p n j"))
+
+        x_bytes = keep.tile([P, S], U8, name="x_bytes", align_bytes=64)
+        nc.vector.tensor_copy(x_bytes[:], byte_table[:].indirect(offs_sb[:]))
+
+        w_codes = keep.tile([P, N], U32, name="w_codes", align_bytes=64)
+        w_bytes = keep.tile([P, N], U8, name="w_bytes", align_bytes=64)
+        nc.vector.quantize_mx(out=w_codes[:].bitcast(FP8X4), scales=w_bytes[:], in_=w_grouped[:].rearrange("p n j -> p (n j)"))
+
+        x_codes = [keep.tile([P, HALF], U32, name=f"x_codes{h}", align_bytes=64) for h in range(S // HALF)]
+        for h in range(S // HALF):
+            nc.vector.tensor_copy(x_codes[h][:], word_table[:].indirect(offs_sb[:, h * HALF // LIST : (h + 1) * HALF // LIST]))
+
+        for h in range(S // HALF):
+            cols = slice(h * HALF, (h + 1) * HALF)
+            for m in range(N // P):
+                rows = slice(m * P, (m + 1) * P)
+                acc = psum.tile([P, HALF], F32, name=f"acc{h}{m}")
+                nc.tensor.matmul_mx(
+                    out=acc[:],
+                    lhsT=w_codes[:, rows].bitcast(FP8X4),
+                    lhsT_scale=w_bytes[:, rows],
+                    rhs=x_codes[h][:].bitcast(FP8X4),
+                    rhs_scale=x_bytes[:, cols],
+                    start=True,
+                    stop=True,
+                )
+                y = keep.tile([P, HALF], F32, name=f"y{h}{m}", align_bytes=64)
+                nc.scalar.copy(y[:], acc[:])
+                scaled = keep.tile([P, HALF], F32, name=f"scaled{h}{m}", align_bytes=64)
+                nc.vector.tensor_tensor(scaled[:], tables[m][:].indirect(task_sb[:, h * HALF // LIST : (h + 1) * HALF // LIST]), y[:], MULT)
+                nc.sync.dma_start(out[rows, cols], scaled[:])

@@ -18,6 +18,8 @@ P = 128
 PACK = 4
 LIST = 16
 HALF = 512
+MM = 256
+TAIL = 128
 
 
 def tile_picked_none_p_kernel(tc, x_words, x_scales, w1, scale, offs, task, out):
@@ -37,7 +39,7 @@ def tile_picked_none_p_kernel(tc, x_words, x_scales, w1, scale, offs, task, out)
         nc.vector.memset(byte_table[:].bitcast(I32), 0)
         nc.sync.dma_start(offs_sb[:], offs)
         for q in range(4):
-            nc.scalar.dma_start(byte_table[32 * q : 32 * q + 4, :].bitcast(I32), x_scales[0, 4 * q : 4 * q + 4, :].bitcast(I32))
+            nc.sync.dma_start(byte_table[32 * q : 32 * q + 4, :].bitcast(I32), x_scales[0, 4 * q : 4 * q + 4, :].bitcast(I32))
         nc.sync.dma_start(w_raw[:], w1.rearrange("(p j) n -> p j n", j=PACK))
         nc.sync.dma_start(word_table[:].bitcast(I32), x_words[0].rearrange("p t r -> p (t r)").bitcast(I32))
         nc.sync.dma_start(task_sb[:], task)
@@ -54,26 +56,47 @@ def tile_picked_none_p_kernel(tc, x_words, x_scales, w1, scale, offs, task, out)
         w_bytes = keep.tile([P, N], U8, name="w_bytes", align_bytes=64)
         nc.vector.quantize_mx(out=w_codes[:].bitcast(FP8X4), scales=w_bytes[:], in_=w_grouped[:].rearrange("p n j -> p (n j)"))
 
-        x_codes = [keep.tile([P, HALF], U32, name=f"x_codes{h}", align_bytes=64) for h in range(S // HALF)]
-        for h in range(S // HALF):
-            nc.vector.tensor_copy(x_codes[h][:], word_table[:].indirect(offs_sb[:, h * HALF // LIST : (h + 1) * HALF // LIST]))
+        cuts = [0,512,1024]
+        x_codes = []
+        for a, b in zip(cuts, cuts[1:]):
+            piece = keep.tile([P, b - a], U32, name=f"x_codes{a}", align_bytes=64)
+            nc.vector.tensor_copy(piece[:], word_table[:].indirect(offs_sb[:, a // LIST : b // LIST]))
+            x_codes.append((a, b, piece))
 
-        for h in range(S // HALF):
-            cols = slice(h * HALF, (h + 1) * HALF)
-            for m in range(N // P):
-                rows = slice(m * P, (m + 1) * P)
-                acc = psum.tile([P, HALF], F32, name=f"acc{h}{m}")
-                nc.tensor.matmul_mx(
-                    out=acc[:],
-                    lhsT=w_codes[:, rows].bitcast(FP8X4),
-                    lhsT_scale=w_bytes[:, rows],
-                    rhs=x_codes[h][:].bitcast(FP8X4),
-                    rhs_scale=x_bytes[:, cols],
-                    start=True,
-                    stop=True,
-                )
-                y = keep.tile([P, HALF], F32, name=f"y{h}{m}", align_bytes=64)
-                nc.scalar.copy(y[:], acc[:])
-                scaled = keep.tile([P, HALF], F32, name=f"scaled{h}{m}", align_bytes=64)
-                nc.vector.tensor_tensor(scaled[:], tables[m][:].indirect(task_sb[:, h * HALF // LIST : (h + 1) * HALF // LIST]), y[:], MULT)
-                nc.sync.dma_start(out[rows, cols], scaled[:])
+        def product(m, a, b):
+            start, piece = [(s, t) for s, e, t in x_codes if s <= a and b <= e][0]
+            rows = slice(m * P, (m + 1) * P)
+            acc = psum.tile([P, b - a], F32, name=f"acc{m}{a}")
+            nc.tensor.matmul_mx(
+                out=acc[:],
+                lhsT=w_codes[:, rows].bitcast(FP8X4),
+                lhsT_scale=w_bytes[:, rows],
+                rhs=piece[:, a - start : b - start].bitcast(FP8X4),
+                rhs_scale=x_bytes[:, a:b],
+                start=True,
+                stop=True,
+            )
+            return acc
+
+        pre = {}
+        for m, a, b in [(0, 896, 1024)]:
+            g = keep.tile([P, b - a], F32, name=f"g{m}{a}", align_bytes=64)
+            nc.vector.tensor_copy(g[:], tables[m][:].indirect(task_sb[:, a // LIST : b // LIST]))
+            pre[(m, a)] = g
+
+        for m, mm, pieces in [(0, [0, 256, 512], [0, 512]), (0, [896, 1024], [896, 1024]), (0, [512, 768, 896], [512, 896]), (1, [0, 512], [0, 512]), (1, [512, 768, 1024], [512, 832, 1024])]:
+            rows = slice(m * P, (m + 1) * P)
+            if (m, mm[0]) in pre:
+                acc = product(m, mm[0], mm[1])
+                scaled = keep.tile([P, mm[1] - mm[0]], F32, name=f"scaled{m}{mm[0]}", align_bytes=64)
+                nc.vector.tensor_tensor(scaled[:], acc[:], pre[(m, mm[0])][:], MULT)
+                nc.sync.dma_start(out[rows, mm[0] : mm[1]], scaled[:])
+                continue
+            y = keep.tile([P, mm[-1] - mm[0]], F32, name=f"y{m}{mm[0]}", align_bytes=64)
+            for a, b in zip(mm, mm[1:]):
+                acc = product(m, a, b)
+                nc.scalar.copy(y[:, a - mm[0] : b - mm[0]], acc[:])
+            for a, b in zip(pieces, pieces[1:]):
+                scaled = keep.tile([P, b - a], F32, name=f"scaled{m}{a}", align_bytes=64)
+                nc.vector.tensor_tensor(scaled[:], tables[m][:].indirect(task_sb[:, a // LIST : b // LIST]), y[:, a - mm[0] : b - mm[0]], MULT)
+                nc.sync.dma_start(out[rows, a:b], scaled[:])

@@ -33,28 +33,31 @@ def tile_picked_none_p_kernel(tc, x_words, x_scales, w1, scale, offs, task, out)
         task_sb = lists.tile([P, S // LIST], U16, name="task_sb")
         byte_table = keep.tile([P, T], U8, name="byte_table", align_bytes=64)
         word_table = keep.tile([P, T], U32, name="word_table", align_bytes=64)
-        w_raw = keep.tile([P, PACK, N], F32, name="w_raw", align_bytes=64)
+        w_raw = [keep.tile([P, PACK, P], F32, name=f"w_raw{m}", align_bytes=64) for m in range(N // P)]
         tables = [keep.tile([P, U], F32, name=f"scale_table{m}", align_bytes=64) for m in range(N // P)]
 
         nc.vector.memset(byte_table[:].bitcast(I32), 0)
         nc.sync.dma_start(offs_sb[:], offs)
+        nc.sync.dma_start(task_sb[:], task)
         for q in range(4):
             nc.sync.dma_start(byte_table[32 * q : 32 * q + 4, :].bitcast(I32), x_scales[0, 4 * q : 4 * q + 4, :].bitcast(I32))
-        nc.sync.dma_start(w_raw[:], w1.rearrange("(p j) n -> p j n", j=PACK))
+        nc.scalar.dma_start(w_raw[0][:], w1[:, 0:P].rearrange("(p j) n -> p j n", j=PACK))
         nc.sync.dma_start(word_table[:].bitcast(I32), x_words[0].rearrange("p t r -> p (t r)").bitcast(I32))
-        nc.sync.dma_start(task_sb[:], task)
+        nc.sync.dma_start(w_raw[1][:], w1[:, P : 2 * P].rearrange("(p j) n -> p j n", j=PACK))
         for m in range(N // P):
             nc.sync.dma_start(tables[m][:], scale[m * P : (m + 1) * P, :])
 
-        w_grouped = keep.tile([P, N, PACK], BF16, name="w_grouped", align_bytes=64)
-        nc.scalar.copy(w_grouped[:], w_raw[:].rearrange("p j n -> p n j"))
+        w_grouped = [keep.tile([P, P, PACK], BF16, name=f"w_grouped{m}", align_bytes=64) for m in range(N // P)]
+        for m in range(N // P):
+            nc.scalar.copy(w_grouped[m][:], w_raw[m][:].rearrange("p j n -> p n j"))
 
         x_bytes = keep.tile([P, S], U8, name="x_bytes", align_bytes=64)
         nc.vector.tensor_copy(x_bytes[:], byte_table[:].indirect(offs_sb[:]))
 
-        w_codes = keep.tile([P, N], U32, name="w_codes", align_bytes=64)
-        w_bytes = keep.tile([P, N], U8, name="w_bytes", align_bytes=64)
-        nc.vector.quantize_mx(out=w_codes[:].bitcast(FP8X4), scales=w_bytes[:], in_=w_grouped[:].rearrange("p n j -> p (n j)"))
+        w_codes = [keep.tile([P, P], U32, name=f"w_codes{m}", align_bytes=64) for m in range(N // P)]
+        w_bytes = [keep.tile([P, P], U8, name=f"w_bytes{m}", align_bytes=64) for m in range(N // P)]
+        for m in range(N // P):
+            nc.vector.quantize_mx(out=w_codes[m][:].bitcast(FP8X4), scales=w_bytes[m][:], in_=w_grouped[m][:].rearrange("p n j -> p (n j)"))
 
         cuts = [0,512,1024]
         x_codes = []
@@ -69,8 +72,8 @@ def tile_picked_none_p_kernel(tc, x_words, x_scales, w1, scale, offs, task, out)
             acc = psum.tile([P, b - a], F32, name=f"acc{m}{a}")
             nc.tensor.matmul_mx(
                 out=acc[:],
-                lhsT=w_codes[:, rows].bitcast(FP8X4),
-                lhsT_scale=w_bytes[:, rows],
+                lhsT=w_codes[m][:].bitcast(FP8X4),
+                lhsT_scale=w_bytes[m][:],
                 rhs=piece[:, a - start : b - start].bitcast(FP8X4),
                 rhs_scale=x_bytes[:, a:b],
                 start=True,

@@ -17,9 +17,6 @@ MULT = mybir.AluOpType.mult
 P = 128
 PACK = 4
 LIST = 16
-HALF = 512
-MM = 256
-TAIL = 128
 
 
 def tile_picked_none_p_kernel(tc, x_words, x_scales, w1, scale, offs, task, out):
@@ -35,40 +32,23 @@ def tile_picked_none_p_kernel(tc, x_words, x_scales, w1, scale, offs, task, out)
         word_table = keep.tile([P, T], U32, name="word_table", align_bytes=64)
         w_raw = [keep.tile([P, PACK, P], F32, name=f"w_raw{m}", align_bytes=64) for m in range(N // P)]
         tables = [keep.tile([P, U], F32, name=f"scale_table{m}", align_bytes=64) for m in range(N // P)]
-
-        nc.vector.memset(byte_table[:].bitcast(I32), 0)
-        nc.sync.dma_start(offs_sb[:], offs)
-        nc.sync.dma_start(task_sb[:], task)
-        for q in range(4):
-            nc.sync.dma_start(byte_table[32 * q : 32 * q + 4, :].bitcast(I32), x_scales[0, 4 * q : 4 * q + 4, :].bitcast(I32))
-        nc.scalar.dma_start(w_raw[0][:], w1[:, 0:P].rearrange("(p j) n -> p j n", j=PACK))
-        nc.sync.dma_start(word_table[:].bitcast(I32), x_words[0].rearrange("p t r -> p (t r)").bitcast(I32))
-        nc.sync.dma_start(w_raw[1][:], w1[:, P : 2 * P].rearrange("(p j) n -> p j n", j=PACK))
-        for m in range(N // P):
-            nc.sync.dma_start(tables[m][:], scale[m * P : (m + 1) * P, :])
-
         w_grouped = [keep.tile([P, P, PACK], BF16, name=f"w_grouped{m}", align_bytes=64) for m in range(N // P)]
-        for m in range(N // P):
-            nc.scalar.copy(w_grouped[m][:], w_raw[m][:].rearrange("p j n -> p n j"))
-
-        x_bytes = keep.tile([P, S], U8, name="x_bytes", align_bytes=64)
-        nc.vector.tensor_copy(x_bytes[:], byte_table[:].indirect(offs_sb[:]))
-
         w_codes = [keep.tile([P, P], U32, name=f"w_codes{m}", align_bytes=64) for m in range(N // P)]
         w_bytes = [keep.tile([P, P], U8, name=f"w_bytes{m}", align_bytes=64) for m in range(N // P)]
-        for m in range(N // P):
+        x_bytes = keep.tile([P, S], U8, name="x_bytes", align_bytes=64)
+
+        def quantize(m):
             nc.vector.quantize_mx(out=w_codes[m][:].bitcast(FP8X4), scales=w_bytes[m][:], in_=w_grouped[m][:].rearrange("p n j -> p (n j)"))
 
-        cuts = [0,512,1024]
         x_codes = []
-        for a, b in zip(cuts, cuts[1:]):
+
+        def gather_words(a, b):
             piece = keep.tile([P, b - a], U32, name=f"x_codes{a}", align_bytes=64)
             nc.vector.tensor_copy(piece[:], word_table[:].indirect(offs_sb[:, a // LIST : b // LIST]))
             x_codes.append((a, b, piece))
 
         def product(m, a, b):
             start, piece = [(s, t) for s, e, t in x_codes if s <= a and b <= e][0]
-            rows = slice(m * P, (m + 1) * P)
             acc = psum.tile([P, b - a], F32, name=f"acc{m}{a}")
             nc.tensor.matmul_mx(
                 out=acc[:],
@@ -81,25 +61,36 @@ def tile_picked_none_p_kernel(tc, x_words, x_scales, w1, scale, offs, task, out)
             )
             return acc
 
-        pre = {}
-        for m, a, b in [(0, 896, 1024)]:
-            g = keep.tile([P, b - a], F32, name=f"g{m}{a}", align_bytes=64)
-            nc.vector.tensor_copy(g[:], tables[m][:].indirect(task_sb[:, a // LIST : b // LIST]))
-            pre[(m, a)] = g
-
-        for m, mm, pieces in [(0, [0, 256, 512], [0, 512]), (0, [896, 1024], [896, 1024]), (0, [512, 768, 896], [512, 896]), (1, [0, 512], [0, 512]), (1, [512, 768, 1024], [512, 832, 1024])]:
+        def finish(m, cuts, pieces):
             rows = slice(m * P, (m + 1) * P)
-            if (m, mm[0]) in pre:
-                acc = product(m, mm[0], mm[1])
-                scaled = keep.tile([P, mm[1] - mm[0]], F32, name=f"scaled{m}{mm[0]}", align_bytes=64)
-                nc.vector.tensor_tensor(scaled[:], acc[:], pre[(m, mm[0])][:], MULT)
-                nc.sync.dma_start(out[rows, mm[0] : mm[1]], scaled[:])
-                continue
-            y = keep.tile([P, mm[-1] - mm[0]], F32, name=f"y{m}{mm[0]}", align_bytes=64)
-            for a, b in zip(mm, mm[1:]):
+            y = keep.tile([P, cuts[-1] - cuts[0]], F32, name=f"y{m}{cuts[0]}", align_bytes=64)
+            for a, b in zip(cuts, cuts[1:]):
                 acc = product(m, a, b)
-                nc.scalar.copy(y[:, a - mm[0] : b - mm[0]], acc[:])
+                nc.scalar.copy(y[:, a - cuts[0] : b - cuts[0]], acc[:])
             for a, b in zip(pieces, pieces[1:]):
                 scaled = keep.tile([P, b - a], F32, name=f"scaled{m}{a}", align_bytes=64)
-                nc.vector.tensor_tensor(scaled[:], tables[m][:].indirect(task_sb[:, a // LIST : b // LIST]), y[:, a - mm[0] : b - mm[0]], MULT)
+                nc.vector.tensor_tensor(scaled[:], tables[m][:].indirect(task_sb[:, a // LIST : b // LIST]), y[:, a - cuts[0] : b - cuts[0]], MULT)
                 nc.sync.dma_start(out[rows, a:b], scaled[:])
+
+        nc.vector.memset(byte_table[:].bitcast(I32), 0)
+        nc.sync.dma_start(w_raw[0][:], w1[:, 0:P].rearrange("(p j) n -> p j n", j=PACK))
+        nc.sync.dma_start(offs_sb[:], offs)
+        nc.sync.dma_start(task_sb[:], task)
+        for r in range(4):
+            nc.sync.dma_start(byte_table[r:P:32, :].bitcast(I32), x_scales[0, r:16:4, :].bitcast(I32))
+        nc.sync.dma_start(word_table[:].bitcast(I32), x_words[0].rearrange("p t r -> p (t r)").bitcast(I32))
+        nc.sync.dma_start(w_raw[1][:], w1[:, P : 2 * P].rearrange("(p j) n -> p j n", j=PACK))
+        for m in range(N // P):
+            nc.sync.dma_start(tables[m][:], scale[m * P : (m + 1) * P, :])
+
+        nc.vector.tensor_copy(w_grouped[0][:], w_raw[0][:].rearrange("p j n -> p n j"))
+        quantize(0)
+        nc.scalar.copy(w_grouped[1][:], w_raw[1][:].rearrange("p j n -> p n j"))
+        nc.vector.tensor_copy(x_bytes[:], byte_table[:].indirect(offs_sb[:]))
+        gather_words(0, 512)
+        quantize(1)
+        gather_words(512, 1024)
+        finish(0, [0, 256, 512], [0, 512])
+        finish(0, [512, 768, 1024], [512, 1024])
+        finish(1, [0, 512], [0, 512])
+        finish(1, [512, 768, 1024], [512, 832, 1024])

@@ -30,7 +30,10 @@ def tile_picked_none_p_kernel(tc, x_words, x_scales, w1, scale, offs, task, out)
         task_sb = lists.tile([P, S // LIST], U16, name="task_sb")
         byte_table = keep.tile([P, T], U8, name="byte_table", align_bytes=64)
         word_table = keep.tile([P, T], U32, name="word_table", align_bytes=64)
-        w_raw = [keep.tile([P, PACK, P], F32, name=f"w_raw{m}", align_bytes=64) for m in range(N // P)]
+        w_early = keep.tile([P, 2, P], F32, name="w_early", align_bytes=64)
+        w_late = keep.tile([P, 2, P], F32, name="w_late", tag="late", align_bytes=64)
+        w_second = keep.tile([P, PACK, P], F32, name="w_second", align_bytes=64)
+        w_rows = w1.rearrange("(p j) n -> p j n", j=PACK)
         tables = [keep.tile([P, U], F32, name=f"scale_table{m}", align_bytes=64) for m in range(N // P)]
         w_grouped = [keep.tile([P, P, PACK], BF16, name=f"w_grouped{m}", align_bytes=64) for m in range(N // P)]
         w_codes = [keep.tile([P, P], U32, name=f"w_codes{m}", align_bytes=64) for m in range(N // P)]
@@ -42,8 +45,8 @@ def tile_picked_none_p_kernel(tc, x_words, x_scales, w1, scale, offs, task, out)
 
         x_codes = []
 
-        def gather_words(a, b):
-            piece = keep.tile([P, b - a], U32, name=f"x_codes{a}", align_bytes=64)
+        def gather_words(a, b, tag):
+            piece = keep.tile([P, b - a], U32, name=f"x_codes{a}", tag=tag, align_bytes=64)
             nc.vector.tensor_copy(piece[:], word_table[:].indirect(offs_sb[:, a // LIST : b // LIST]))
             x_codes.append((a, b, piece))
 
@@ -61,36 +64,39 @@ def tile_picked_none_p_kernel(tc, x_words, x_scales, w1, scale, offs, task, out)
             )
             return acc
 
-        def finish(m, cuts, pieces):
-            rows = slice(m * P, (m + 1) * P)
+        def finish(m, cuts, pieces, scaled):
             y = keep.tile([P, cuts[-1] - cuts[0]], F32, name=f"y{m}{cuts[0]}", align_bytes=64)
             for a, b in zip(cuts, cuts[1:]):
                 acc = product(m, a, b)
                 nc.scalar.copy(y[:, a - cuts[0] : b - cuts[0]], acc[:])
             for a, b in zip(pieces, pieces[1:]):
-                scaled = keep.tile([P, b - a], F32, name=f"scaled{m}{a}", align_bytes=64)
-                nc.vector.tensor_tensor(scaled[:], tables[m][:].indirect(task_sb[:, a // LIST : b // LIST]), y[:, a - cuts[0] : b - cuts[0]], MULT)
-                nc.sync.dma_start(out[rows, a:b], scaled[:])
+                nc.vector.tensor_tensor(scaled[:, a:b], tables[m][:].indirect(task_sb[:, a // LIST : b // LIST]), y[:, a - cuts[0] : b - cuts[0]], MULT)
+                if m == 1:
+                    nc.sync.dma_start(out[P:N, a:b], scaled[:, a:b])
 
         nc.vector.memset(byte_table[:].bitcast(I32), 0)
-        nc.sync.dma_start(w_raw[0][:], w1[:, 0:P].rearrange("(p j) n -> p j n", j=PACK))
+        nc.sync.dma_start(w_early[:], w_rows[:, 0:2, 0:P])
         nc.sync.dma_start(offs_sb[:], offs)
         nc.sync.dma_start(task_sb[:], task)
         for r in range(4):
             nc.sync.dma_start(byte_table[r:P:32, :].bitcast(I32), x_scales[0, r:16:4, :].bitcast(I32))
         nc.sync.dma_start(word_table[:].bitcast(I32), x_words[0].rearrange("p t r -> p (t r)").bitcast(I32))
-        nc.sync.dma_start(w_raw[1][:], w1[:, P : 2 * P].rearrange("(p j) n -> p j n", j=PACK))
+        nc.sync.dma_start(w_late[:], w_rows[:, 2:4, 0:P])
+        nc.sync.dma_start(w_second[:], w_rows[:, :, P:N])
         for m in range(N // P):
             nc.sync.dma_start(tables[m][:], scale[m * P : (m + 1) * P, :])
 
-        nc.vector.tensor_copy(w_grouped[0][:], w_raw[0][:].rearrange("p j n -> p n j"))
-        quantize(0)
-        nc.scalar.copy(w_grouped[1][:], w_raw[1][:].rearrange("p j n -> p n j"))
+        nc.vector.tensor_copy(w_grouped[0][:, :, 0:2], w_early[:].rearrange("p j n -> p n j"))
         nc.vector.tensor_copy(x_bytes[:], byte_table[:].indirect(offs_sb[:]))
-        gather_words(0, 512)
+        gather_words(0, 512, "first")
+        nc.scalar.copy(w_grouped[0][:, :, 2:4], w_late[:].rearrange("p j n -> p n j"))
+        quantize(0)
+        nc.scalar.copy(w_grouped[1][:], w_second[:].rearrange("p j n -> p n j"))
+        gather_words(512, 1024, "late")
         quantize(1)
-        gather_words(512, 1024)
-        finish(0, [0, 256, 512], [0, 512])
-        finish(0, [512, 768, 1024], [512, 1024])
-        finish(1, [0, 512], [0, 512])
-        finish(1, [512, 768, 1024], [512, 832, 1024])
+        scaled = [keep.tile([P, S], F32, name=f"scaled{m}", align_bytes=64) for m in range(N // P)]
+        finish(0, [0, 256, 512], [0, 512], scaled[0])
+        finish(0, [512, 768, 1024], [512, 1024], scaled[0])
+        nc.sync.dma_start(out[0:P, :], scaled[0][:])
+        finish(1, [0, 512], [0, 512], scaled[1])
+        finish(1, [512, 768, 1024], [512, 832, 1024], scaled[1])

@@ -99,4 +99,4 @@ def tile_picked_none_p_kernel(tc, x_words, x_scales, w1, scale, offs, task, out)
         finish(0, [512, 768, 1024], [512, 1024], scaled[0])
         nc.sync.dma_start(out[0:P, :], scaled[0][:])
         finish(1, [0, 512], [0, 512], scaled[1])
-        finish(1, [512, 768, 1024], [512, 832, 1024], scaled[1])
+        finish(1, [512, 768, 1024], [512, 768, 1024], scaled[1])

@@ -77,12 +77,12 @@ def tile_picked_none_p_kernel(tc, x_words, x_scales, w1, scale, offs, task, out)
         nc.vector.memset(byte_table[:].bitcast(I32), 0)
         nc.sync.dma_start(w_early[:], w_rows[:, 0:2, 0:P])
         nc.sync.dma_start(offs_sb[:], offs)
-        nc.sync.dma_start(task_sb[:], task)
         for r in range(4):
             nc.sync.dma_start(byte_table[r:P:32, :].bitcast(I32), x_scales[0, r:16:4, :].bitcast(I32))
         nc.sync.dma_start(word_table[:].bitcast(I32), x_words[0].rearrange("p t r -> p (t r)").bitcast(I32))
         nc.sync.dma_start(w_late[:], w_rows[:, 2:4, 0:P])
         nc.sync.dma_start(w_second[:], w_rows[:, :, P:N])
+        nc.sync.dma_start(task_sb[:], task)
         for m in range(N // P):
             nc.sync.dma_start(tables[m][:], scale[m * P : (m + 1) * P, :])
 

@@ -16,11 +16,16 @@ MULT = mybir.AluOpType.mult
 
 P = 128
 PACK = 4
+QUADRANT = 32
 LIST = 16
+HALF = S // 2
+QUARTER = S // 4
+PAIR = PACK // 2
 
 
 def tile_picked_none_p_kernel(tc, x_words, x_scales, w1, scale, offs, task, out):
     nc = tc.nc
+    blocks = range(N // P)
     with ExitStack() as ctx:
         lists = ctx.enter_context(tc.tile_pool(name="lists", bufs=1))
         keep = ctx.enter_context(tc.tile_pool(name="keep", bufs=1))
@@ -30,73 +35,78 @@ def tile_picked_none_p_kernel(tc, x_words, x_scales, w1, scale, offs, task, out)
         task_sb = lists.tile([P, S // LIST], U16, name="task_sb")
         byte_table = keep.tile([P, T], U8, name="byte_table", align_bytes=64)
         word_table = keep.tile([P, T], U32, name="word_table", align_bytes=64)
-        w_early = keep.tile([P, 2, P], F32, name="w_early", align_bytes=64)
-        w_late = keep.tile([P, 2, P], F32, name="w_late", tag="late", align_bytes=64)
+        w_early = keep.tile([P, PAIR, P], F32, name="w_early", align_bytes=64)
+        w_late = keep.tile([P, PAIR, P], F32, name="w_late", tag="late_slot", align_bytes=64)
         w_second = keep.tile([P, PACK, P], F32, name="w_second", align_bytes=64)
-        w_rows = w1.rearrange("(p j) n -> p j n", j=PACK)
-        tables = [keep.tile([P, U], F32, name=f"scale_table{m}", align_bytes=64) for m in range(N // P)]
-        w_grouped = [keep.tile([P, P, PACK], BF16, name=f"w_grouped{m}", align_bytes=64) for m in range(N // P)]
-        w_codes = [keep.tile([P, P], U32, name=f"w_codes{m}", align_bytes=64) for m in range(N // P)]
-        w_bytes = [keep.tile([P, P], U8, name=f"w_bytes{m}", align_bytes=64) for m in range(N // P)]
+        scale_tables = [keep.tile([P, U], F32, name=f"scale_table{m}", align_bytes=64) for m in blocks]
+        w_grouped = [keep.tile([P, P, PACK], BF16, name=f"w_grouped{m}", align_bytes=64) for m in blocks]
+        w_codes = [keep.tile([P, P], U32, name=f"w_codes{m}", align_bytes=64) for m in blocks]
+        w_bytes = [keep.tile([P, P], U8, name=f"w_bytes{m}", align_bytes=64) for m in blocks]
         x_bytes = keep.tile([P, S], U8, name="x_bytes", align_bytes=64)
+
+        def entries(list_tile, a, b):
+            return list_tile[:, a // LIST : b // LIST]
 
         def quantize(m):
             nc.vector.quantize_mx(out=w_codes[m][:].bitcast(FP8X4), scales=w_bytes[m][:], in_=w_grouped[m][:].rearrange("p n j -> p (n j)"))
 
-        x_codes = []
+        def gather_words(start, tag):
+            x_codes = keep.tile([P, HALF], U32, name=f"x_codes{start}", tag=tag, align_bytes=64)
+            nc.vector.tensor_copy(x_codes[:], word_table[:].indirect(entries(offs_sb, start, start + HALF)))
+            return x_codes
 
-        def gather_words(a, b, tag):
-            piece = keep.tile([P, b - a], U32, name=f"x_codes{a}", tag=tag, align_bytes=64)
-            nc.vector.tensor_copy(piece[:], word_table[:].indirect(offs_sb[:, a // LIST : b // LIST]))
-            x_codes.append((a, b, piece))
+        def products(m, start, x_codes, width):
+            y = keep.tile([P, HALF], F32, name=f"y{m}_{start}", align_bytes=64)
+            for a in range(0, HALF, width):
+                acc = psum.tile([P, width], F32, name=f"acc{m}_{start + a}")
+                nc.tensor.matmul_mx(
+                    out=acc[:],
+                    lhsT=w_codes[m][:].bitcast(FP8X4),
+                    lhsT_scale=w_bytes[m][:],
+                    rhs=x_codes[:, a : a + width].bitcast(FP8X4),
+                    rhs_scale=x_bytes[:, start + a : start + a + width],
+                    start=True,
+                    stop=True,
+                )
+                nc.scalar.copy(y[:, a : a + width], acc[:])
+            return y
 
-        def product(m, a, b):
-            start, piece = [(s, t) for s, e, t in x_codes if s <= a and b <= e][0]
-            acc = psum.tile([P, b - a], F32, name=f"acc{m}{a}")
-            nc.tensor.matmul_mx(
-                out=acc[:],
-                lhsT=w_codes[m][:].bitcast(FP8X4),
-                lhsT_scale=w_bytes[m][:],
-                rhs=piece[:, a - start : b - start].bitcast(FP8X4),
-                rhs_scale=x_bytes[:, a:b],
-                start=True,
-                stop=True,
-            )
-            return acc
-
-        def finish(m, cuts, pieces, scaled):
-            y = keep.tile([P, cuts[-1] - cuts[0]], F32, name=f"y{m}{cuts[0]}", align_bytes=64)
-            for a, b in zip(cuts, cuts[1:]):
-                acc = product(m, a, b)
-                nc.scalar.copy(y[:, a - cuts[0] : b - cuts[0]], acc[:])
-            for a, b in zip(pieces, pieces[1:]):
-                nc.vector.tensor_tensor(scaled[:, a:b], tables[m][:].indirect(task_sb[:, a // LIST : b // LIST]), y[:, a - cuts[0] : b - cuts[0]], MULT)
-                if m == 1:
-                    nc.sync.dma_start(out[P:N, a:b], scaled[:, a:b])
+        def scale_columns(m, a, b, y_columns):
+            nc.vector.tensor_tensor(scaled[m][:, a:b], scale_tables[m][:].indirect(entries(task_sb, a, b)), y_columns, MULT)
 
         nc.vector.memset(byte_table[:].bitcast(I32), 0)
-        nc.sync.dma_start(w_early[:], w_rows[:, 0:2, 0:P])
+
+        w_rows = w1.rearrange("(p j) n -> p j n", j=PACK)
+        nc.sync.dma_start(w_early[:], w_rows[:, 0:PAIR, 0:P])
         nc.sync.dma_start(offs_sb[:], offs)
-        for r in range(4):
-            nc.sync.dma_start(byte_table[r:P:32, :].bitcast(I32), x_scales[0, r:16:4, :].bitcast(I32))
+        for r in range(PACK):
+            queue = nc.scalar if r == PACK - 1 else nc.sync
+            queue.dma_start(byte_table[r:P:QUADRANT, :].bitcast(I32), x_scales[0, r::PACK, :].bitcast(I32))
         nc.sync.dma_start(word_table[:].bitcast(I32), x_words[0].rearrange("p t r -> p (t r)").bitcast(I32))
-        nc.sync.dma_start(w_late[:], w_rows[:, 2:4, 0:P])
+        nc.sync.dma_start(w_late[:], w_rows[:, PAIR:PACK, 0:P])
         nc.sync.dma_start(w_second[:], w_rows[:, :, P:N])
         nc.sync.dma_start(task_sb[:], task)
-        for m in range(N // P):
-            nc.sync.dma_start(tables[m][:], scale[m * P : (m + 1) * P, :])
+        for m in blocks:
+            nc.sync.dma_start(scale_tables[m][:], scale[m * P : (m + 1) * P, :])
 
-        nc.vector.tensor_copy(w_grouped[0][:, :, 0:2], w_early[:].rearrange("p j n -> p n j"))
+        nc.vector.tensor_copy(w_grouped[0][:, :, 0:PAIR], w_early[:].rearrange("p j n -> p n j"))
         nc.vector.tensor_copy(x_bytes[:], byte_table[:].indirect(offs_sb[:]))
-        gather_words(0, 512, "first")
-        nc.scalar.copy(w_grouped[0][:, :, 2:4], w_late[:].rearrange("p j n -> p n j"))
+        first_codes = gather_words(0, "first_slot")
+        nc.scalar.copy(w_grouped[0][:, :, PAIR:PACK], w_late[:].rearrange("p j n -> p n j"))
         quantize(0)
         nc.scalar.copy(w_grouped[1][:], w_second[:].rearrange("p j n -> p n j"))
-        gather_words(512, 1024, "late")
+        second_codes = gather_words(HALF, "late_slot")
         quantize(1)
-        scaled = [keep.tile([P, S], F32, name=f"scaled{m}", align_bytes=64) for m in range(N // P)]
-        finish(0, [0, 256, 512], [0, 512], scaled[0])
-        finish(0, [512, 768, 1024], [512, 1024], scaled[0])
+
+        scaled = [keep.tile([P, S], F32, name=f"scaled{m}", align_bytes=64) for m in blocks]
+
+        for start, x_codes in ((0, first_codes), (HALF, second_codes)):
+            scale_columns(0, start, start + HALF, products(0, start, x_codes, QUARTER)[:])
         nc.sync.dma_start(out[0:P, :], scaled[0][:])
-        finish(1, [0, 512], [0, 512], scaled[1])
-        finish(1, [512, 768, 1024], [512, 768, 1024], scaled[1])
+
+        scale_columns(1, 0, HALF, products(1, 0, first_codes, HALF)[:])
+        nc.sync.dma_start(out[P:N, 0:HALF], scaled[1][:, 0:HALF])
+        y_last = products(1, HALF, second_codes, QUARTER)
+        for a in range(HALF, S, QUARTER):
+            scale_columns(1, a, a + QUARTER, y_last[:, a - HALF : a - HALF + QUARTER])
+            nc.sync.dma_start(out[P:N, a : a + QUARTER], scaled[1][:, a : a + QUARTER])

@@ -18,6 +18,7 @@ P = 128
 PACK = 4
 QUADRANT = 32
 LIST = 16
+ROW_STEP = 8
 HALF = S // 2
 QUARTER = S // 4
 PAIR = PACK // 2
@@ -33,22 +34,26 @@ def tile_picked_none_p_kernel(tc, x_words, x_scales, w1, scale, offs, task, out)
 
         offs_sb = lists.tile([P, S // LIST], U16, name="offs_sb")
         task_sb = lists.tile([P, S // LIST], U16, name="task_sb")
-        byte_table = keep.tile([P, T], U8, name="byte_table", align_bytes=64)
+        byte_table = keep.tile([P, T], U8, name="byte_table", tag="byte_slot", align_bytes=64)
         word_table = keep.tile([P, T], U32, name="word_table", align_bytes=64)
-        w_early = keep.tile([P, PAIR, P], F32, name="w_early", align_bytes=64)
-        w_late = keep.tile([P, PAIR, P], F32, name="w_late", tag="late_slot", align_bytes=64)
-        w_second = keep.tile([P, PACK, P], F32, name="w_second", align_bytes=64)
-        scale_tables = [keep.tile([P, U], F32, name=f"scale_table{m}", align_bytes=64) for m in blocks]
+        w_early = keep.tile([P, PAIR, N], F32, name="w_early", tag="early_slot", align_bytes=64)
+        w_late = keep.tile([P, PAIR, N], F32, name="w_late", tag="late_slot", align_bytes=64)
         w_grouped = [keep.tile([P, P, PACK], BF16, name=f"w_grouped{m}", align_bytes=64) for m in blocks]
         w_codes = [keep.tile([P, P], U32, name=f"w_codes{m}", align_bytes=64) for m in blocks]
         w_bytes = [keep.tile([P, P], U8, name=f"w_bytes{m}", align_bytes=64) for m in blocks]
-        x_bytes = keep.tile([P, S], U8, name="x_bytes", align_bytes=64)
+        picked_bytes = [keep.tile([P, HALF], U8, name=f"picked_bytes{h}", align_bytes=64) for h in range(2)]
+        x_bytes = [keep.tile([P, HALF], U8, name=f"x_bytes{h}", align_bytes=64) for h in range(2)]
+        scale_tables = []
 
         def entries(list_tile, a, b):
             return list_tile[:, a // LIST : b // LIST]
 
         def quantize(m):
             nc.vector.quantize_mx(out=w_codes[m][:].bitcast(FP8X4), scales=w_bytes[m][:], in_=w_grouped[m][:].rearrange("p n j -> p (n j)"))
+
+        def place_bytes(h):
+            for r in range(PACK):
+                nc.sync.dma_start(x_bytes[h][r:P:QUADRANT, :].bitcast(I32), picked_bytes[h][r * ROW_STEP : P : QUADRANT, :].bitcast(I32))
 
         def gather_words(start, tag):
             x_codes = keep.tile([P, HALF], U32, name=f"x_codes{start}", tag=tag, align_bytes=64)
@@ -64,7 +69,7 @@ def tile_picked_none_p_kernel(tc, x_words, x_scales, w1, scale, offs, task, out)
                     lhsT=w_codes[m][:].bitcast(FP8X4),
                     lhsT_scale=w_bytes[m][:],
                     rhs=x_codes[:, a : a + width].bitcast(FP8X4),
-                    rhs_scale=x_bytes[:, start + a : start + a + width],
+                    rhs_scale=x_bytes[start // HALF][:, a : a + width],
                     start=True,
                     stop=True,
                 )
@@ -77,36 +82,43 @@ def tile_picked_none_p_kernel(tc, x_words, x_scales, w1, scale, offs, task, out)
         nc.vector.memset(byte_table[:].bitcast(I32), 0)
 
         w_rows = w1.rearrange("(p j) n -> p j n", j=PACK)
-        nc.sync.dma_start(w_early[:], w_rows[:, 0:PAIR, 0:P])
+        nc.sync.dma_start(w_early[:], w_rows[:, 0:PAIR, :])
         nc.sync.dma_start(offs_sb[:], offs)
-        for r in range(PACK):
-            queue = nc.scalar if r == PACK - 1 else nc.sync
-            queue.dma_start(byte_table[r:P:QUADRANT, :].bitcast(I32), x_scales[0, r::PACK, :].bitcast(I32))
+        nc.sync.dma_start(byte_table[0:P:ROW_STEP, :].bitcast(I32), x_scales[0].bitcast(I32))
         nc.sync.dma_start(word_table[:].bitcast(I32), x_words[0].rearrange("p t r -> p (t r)").bitcast(I32))
-        nc.sync.dma_start(w_late[:], w_rows[:, PAIR:PACK, 0:P])
-        nc.sync.dma_start(w_second[:], w_rows[:, :, P:N])
+        nc.sync.dma_start(w_late[:], w_rows[:, PAIR:PACK, :])
         nc.sync.dma_start(task_sb[:], task)
-        for m in blocks:
-            nc.sync.dma_start(scale_tables[m][:], scale[m * P : (m + 1) * P, :])
 
-        nc.vector.tensor_copy(w_grouped[0][:, :, 0:PAIR], w_early[:].rearrange("p j n -> p n j"))
-        nc.vector.tensor_copy(x_bytes[:], byte_table[:].indirect(offs_sb[:]))
+        for m in blocks:
+            nc.scalar.copy(w_grouped[m][:, :, 0:PAIR], w_early[:, :, m * P : (m + 1) * P].rearrange("p j n -> p n j"))
+        for h in range(2):
+            nc.vector.tensor_copy(picked_bytes[h][:], byte_table[:].indirect(entries(offs_sb, h * HALF, (h + 1) * HALF)))
+        place_bytes(0)
+        for m in blocks:
+            scale_tables.append(keep.tile([P, U], F32, name=f"scale_table{m}", tag=("early_slot", "byte_slot")[m], align_bytes=64))
+            nc.sync.dma_start(scale_tables[m][:], scale[m * P : (m + 1) * P, :])
+        place_bytes(1)
+
         first_codes = gather_words(0, "first_slot")
-        nc.scalar.copy(w_grouped[0][:, :, PAIR:PACK], w_late[:].rearrange("p j n -> p n j"))
-        quantize(0)
-        nc.scalar.copy(w_grouped[1][:], w_second[:].rearrange("p j n -> p n j"))
+        for m in blocks:
+            nc.scalar.copy(w_grouped[m][:, :, PAIR:PACK], w_late[:, :, m * P : (m + 1) * P].rearrange("p j n -> p n j"))
+        for m in blocks:
+            quantize(m)
         second_codes = gather_words(HALF, "late_slot")
-        quantize(1)
 
         scaled = [keep.tile([P, S], F32, name=f"scaled{m}", align_bytes=64) for m in blocks]
 
-        for start, x_codes in ((0, first_codes), (HALF, second_codes)):
-            scale_columns(0, start, start + HALF, products(0, start, x_codes, QUARTER)[:])
-        nc.sync.dma_start(out[0:P, :], scaled[0][:])
+        def store(m, a, b):
+            for c in range(a, b, QUARTER):
+                nc.sync.dma_start(out[m * P : (m + 1) * P, c : c + QUARTER], scaled[m][:, c : c + QUARTER])
 
+        scale_columns(0, 0, HALF, products(0, 0, first_codes, QUARTER)[:])
+        store(0, 0, HALF)
         scale_columns(1, 0, HALF, products(1, 0, first_codes, HALF)[:])
-        nc.sync.dma_start(out[P:N, 0:HALF], scaled[1][:, 0:HALF])
+        store(1, 0, HALF)
+        scale_columns(0, HALF, S, products(0, HALF, second_codes, QUARTER)[:])
+        store(0, HALF, S)
         y_last = products(1, HALF, second_codes, QUARTER)
         for a in range(HALF, S, QUARTER):
             scale_columns(1, a, a + QUARTER, y_last[:, a - HALF : a - HALF + QUARTER])
-            nc.sync.dma_start(out[P:N, a : a + QUARTER], scaled[1][:, a : a + QUARTER])
+            store(1, a, a + QUARTER)

@@ -19,7 +19,7 @@ PACK = 4
 QUADRANT = 32
 LIST = 16
 ROW_STEP = 8
-HALF = S // 2
+FIRST = 640
 QUARTER = S // 4
 PAIR = PACK // 2
 
@@ -41,8 +41,9 @@ def tile_picked_none_p_kernel(tc, x_words, x_scales, w1, scale, offs, task, out)
         w_grouped = [keep.tile([P, P, PACK], BF16, name=f"w_grouped{m}", align_bytes=64) for m in blocks]
         w_codes = [keep.tile([P, P], U32, name=f"w_codes{m}", align_bytes=64) for m in blocks]
         w_bytes = [keep.tile([P, P], U8, name=f"w_bytes{m}", align_bytes=64) for m in blocks]
-        picked_bytes = [keep.tile([P, HALF], U8, name=f"picked_bytes{h}", align_bytes=64) for h in range(2)]
-        x_bytes = [keep.tile([P, HALF], U8, name=f"x_bytes{h}", align_bytes=64) for h in range(2)]
+        parts = ((0, FIRST), (FIRST, S))
+        picked_bytes = [keep.tile([P, b - a], U8, name=f"picked_bytes{a}", align_bytes=64) for a, b in parts]
+        x_bytes = [keep.tile([P, b - a], U8, name=f"x_bytes{a}", align_bytes=64) for a, b in parts]
         scale_tables = []
 
         def entries(list_tile, a, b):
@@ -55,21 +56,24 @@ def tile_picked_none_p_kernel(tc, x_words, x_scales, w1, scale, offs, task, out)
             for r in range(PACK):
                 nc.sync.dma_start(x_bytes[h][r:P:QUADRANT, :].bitcast(I32), picked_bytes[h][r * ROW_STEP : P : QUADRANT, :].bitcast(I32))
 
-        def gather_words(start, tag):
-            x_codes = keep.tile([P, HALF], U32, name=f"x_codes{start}", tag=tag, align_bytes=64)
-            nc.vector.tensor_copy(x_codes[:], word_table[:].indirect(entries(offs_sb, start, start + HALF)))
+        def gather_words(h, tag):
+            start, end = parts[h]
+            x_codes = keep.tile([P, end - start], U32, name=f"x_codes{start}", tag=tag, align_bytes=64)
+            nc.vector.tensor_copy(x_codes[:], word_table[:].indirect(entries(offs_sb, start, end)))
             return x_codes
 
-        def products(m, start, x_codes, width):
-            y = keep.tile([P, HALF], F32, name=f"y{m}_{start}", align_bytes=64)
-            for a in range(0, HALF, width):
-                acc = psum.tile([P, width], F32, name=f"acc{m}_{start + a}")
+        def products(m, h, x_codes, widths):
+            start, end = parts[h]
+            y = keep.tile([P, end - start], F32, name=f"y{m}_{start}", align_bytes=64)
+            for i, width in enumerate(widths):
+                a = sum(widths[:i])
+                acc = psum.tile([P, width], F32, name=f"acc{m}_{start + a}", tag=f"bank{(3 * (m + 2 * h) + i) % 8}")
                 nc.tensor.matmul_mx(
                     out=acc[:],
                     lhsT=w_codes[m][:].bitcast(FP8X4),
                     lhsT_scale=w_bytes[m][:],
                     rhs=x_codes[:, a : a + width].bitcast(FP8X4),
-                    rhs_scale=x_bytes[start // HALF][:, a : a + width],
+                    rhs_scale=x_bytes[h][:, a : a + width],
                     start=True,
                     stop=True,
                 )
@@ -92,7 +96,7 @@ def tile_picked_none_p_kernel(tc, x_words, x_scales, w1, scale, offs, task, out)
         for m in blocks:
             nc.scalar.copy(w_grouped[m][:, :, 0:PAIR], w_early[:, :, m * P : (m + 1) * P].rearrange("p j n -> p n j"))
         for h in range(2):
-            nc.vector.tensor_copy(picked_bytes[h][:], byte_table[:].indirect(entries(offs_sb, h * HALF, (h + 1) * HALF)))
+            nc.vector.tensor_copy(picked_bytes[h][:], byte_table[:].indirect(entries(offs_sb, *parts[h])))
         place_bytes(0)
         for m in blocks:
             scale_tables.append(keep.tile([P, U], F32, name=f"scale_table{m}", tag=("early_slot", "byte_slot")[m], align_bytes=64))
@@ -104,21 +108,24 @@ def tile_picked_none_p_kernel(tc, x_words, x_scales, w1, scale, offs, task, out)
             nc.scalar.copy(w_grouped[m][:, :, PAIR:PACK], w_late[:, :, m * P : (m + 1) * P].rearrange("p j n -> p n j"))
         for m in blocks:
             quantize(m)
-        second_codes = gather_words(HALF, "late_slot")
+        second_codes = gather_words(1, "late_slot")
 
         scaled = [keep.tile([P, S], F32, name=f"scaled{m}", align_bytes=64) for m in blocks]
 
         def store(m, a, b):
-            for c in range(a, b, QUARTER):
-                nc.sync.dma_start(out[m * P : (m + 1) * P, c : c + QUARTER], scaled[m][:, c : c + QUARTER])
+            nc.sync.dma_start(out[m * P : (m + 1) * P, a:b], scaled[m][:, a:b])
 
-        scale_columns(0, 0, HALF, products(0, 0, first_codes, QUARTER)[:])
-        store(0, 0, HALF)
-        scale_columns(1, 0, HALF, products(1, 0, first_codes, HALF)[:])
-        store(1, 0, HALF)
-        scale_columns(0, HALF, S, products(0, HALF, second_codes, QUARTER)[:])
-        store(0, HALF, S)
-        y_last = products(1, HALF, second_codes, QUARTER)
-        for a in range(HALF, S, QUARTER):
-            scale_columns(1, a, a + QUARTER, y_last[:, a - HALF : a - HALF + QUARTER])
-            store(1, a, a + QUARTER)
+        for m in blocks:
+            y = products(m, 0, first_codes, (256, 256, 128))
+            for a, b in ((0, QUARTER), (QUARTER, FIRST)) if m == 0 else ((0, FIRST),):
+                scale_columns(m, a, b, y[:, a:b])
+            store(m, 0, FIRST // 2)
+            store(m, FIRST // 2, FIRST)
+        middle = (FIRST + S) // 2
+        scale_columns(0, FIRST, S, products(0, 1, second_codes, (256, 128))[:])
+        store(0, FIRST, middle)
+        store(0, middle, S)
+        y_last = products(1, 1, second_codes, (256, 128))
+        for a, b in ((FIRST, middle), (middle, S)):
+            scale_columns(1, a, b, y_last[:, a - FIRST : b - FIRST])
+            store(1, a, b)

@@ -30,14 +30,16 @@ def tile_picked_none_p_kernel(tc, x_words, x_scales, w1, scale, offs, task, out)
     with ExitStack() as ctx:
         lists = ctx.enter_context(tc.tile_pool(name="lists", bufs=1))
         keep = ctx.enter_context(tc.tile_pool(name="keep", bufs=1))
+        shared = ctx.enter_context(tc.tile_pool(name="shared", bufs=1))
         psum = ctx.enter_context(tc.psum_pool(name="psum", bufs=1))
 
         offs_sb = lists.tile([P, S // LIST], U16, name="offs_sb")
         task_sb = lists.tile([P, S // LIST], U16, name="task_sb")
-        byte_table = keep.tile([P, T], U8, name="byte_table", tag="byte_slot", align_bytes=64)
+        byte_table = shared.tile([P, T], U8, name="byte_table", offset=4 * U - T // 2, align_bytes=64)
         word_table = keep.tile([P, T], U32, name="word_table", align_bytes=64)
-        w_early = keep.tile([P, PAIR, N], F32, name="w_early", tag="early_slot", align_bytes=64)
-        w_late = keep.tile([P, PAIR, N], F32, name="w_late", tag="late_slot", align_bytes=64)
+        w_early = keep.tile([P, PAIR, P], F32, name="w_early", align_bytes=64)
+        w_late = keep.tile([P, PAIR, P], F32, name="w_late", tag="late_slot", align_bytes=64)
+        w_second = keep.tile([P, PACK, P], F32, name="w_second", align_bytes=64)
         w_grouped = [keep.tile([P, P, PACK], BF16, name=f"w_grouped{m}", align_bytes=64) for m in blocks]
         w_codes = [keep.tile([P, P], U32, name=f"w_codes{m}", align_bytes=64) for m in blocks]
         w_bytes = [keep.tile([P, P], U8, name=f"w_bytes{m}", align_bytes=64) for m in blocks]
@@ -86,29 +88,29 @@ def tile_picked_none_p_kernel(tc, x_words, x_scales, w1, scale, offs, task, out)
         nc.vector.memset(byte_table[:].bitcast(I32), 0)
 
         w_rows = w1.rearrange("(p j) n -> p j n", j=PACK)
-        nc.sync.dma_start(w_early[:], w_rows[:, 0:PAIR, :])
+        nc.sync.dma_start(w_early[:], w_rows[:, 0:PAIR, 0:P])
         nc.sync.dma_start(offs_sb[:], offs)
         nc.sync.dma_start(byte_table[0:P:ROW_STEP, :].bitcast(I32), x_scales[0].bitcast(I32))
         nc.sync.dma_start(word_table[:].bitcast(I32), x_words[0].rearrange("p t r -> p (t r)").bitcast(I32))
-        nc.sync.dma_start(w_late[:], w_rows[:, PAIR:PACK, :])
+        nc.sync.dma_start(w_late[:], w_rows[:, PAIR:PACK, 0:P])
+        nc.sync.dma_start(w_second[:], w_rows[:, :, P:N])
         nc.sync.dma_start(task_sb[:], task)
 
-        for m in blocks:
-            nc.scalar.copy(w_grouped[m][:, :, 0:PAIR], w_early[:, :, m * P : (m + 1) * P].rearrange("p j n -> p n j"))
+        nc.scalar.copy(w_grouped[0][:, :, 0:PAIR], w_early[:].rearrange("p j n -> p n j"))
         for h in range(2):
             nc.vector.tensor_copy(picked_bytes[h][:], byte_table[:].indirect(entries(offs_sb, *parts[h])))
         place_bytes(0)
         for m in blocks:
-            scale_tables.append(keep.tile([P, U], F32, name=f"scale_table{m}", tag=("early_slot", "byte_slot")[m], align_bytes=64))
+            scale_tables.append(shared.tile([P, U], F32, name=f"scale_table{m}", offset=4 * U * m, align_bytes=64))
             nc.sync.dma_start(scale_tables[m][:], scale[m * P : (m + 1) * P, :])
         place_bytes(1)
 
         first_codes = gather_words(0, "first_slot")
-        for m in blocks:
-            nc.scalar.copy(w_grouped[m][:, :, PAIR:PACK], w_late[:, :, m * P : (m + 1) * P].rearrange("p j n -> p n j"))
-        for m in blocks:
-            quantize(m)
+        nc.scalar.copy(w_grouped[0][:, :, PAIR:PACK], w_late[:].rearrange("p j n -> p n j"))
+        quantize(0)
+        nc.scalar.copy(w_grouped[1][:], w_second[:].rearrange("p j n -> p n j"))
         second_codes = gather_words(1, "late_slot")
+        quantize(1)
 
         scaled = [keep.tile([P, S], F32, name=f"scaled{m}", align_bytes=64) for m in blocks]
 
@@ -123,8 +125,7 @@ def tile_picked_none_p_kernel(tc, x_words, x_scales, w1, scale, offs, task, out)
             store(m, FIRST // 2, FIRST)
         middle = (FIRST + S) // 2
         scale_columns(0, FIRST, S, products(0, 1, second_codes, (256, 128))[:])
-        store(0, FIRST, middle)
-        store(0, middle, S)
+        store(0, FIRST, S)
         y_last = products(1, 1, second_codes, (256, 128))
         for a, b in ((FIRST, middle), (middle, S)):
             scale_columns(1, a, b, y_last[:, a - FIRST : b - FIRST])

@@ -20,6 +20,7 @@ QUADRANT = 32
 LIST = 16
 ROW_STEP = 8
 FIRST = 640
+HALF = S // 2
 QUARTER = S // 4
 PAIR = PACK // 2
 
@@ -58,32 +59,28 @@ def tile_picked_none_p_kernel(tc, x_words, x_scales, w1, scale, offs, task, out)
             for r in range(PACK):
                 nc.sync.dma_start(x_bytes[h][r:P:QUADRANT, :].bitcast(I32), picked_bytes[h][r * ROW_STEP : P : QUADRANT, :].bitcast(I32))
 
-        def gather_words(h, tag):
-            start, end = parts[h]
-            x_codes = keep.tile([P, end - start], U32, name=f"x_codes{start}", tag=tag, align_bytes=64)
-            nc.vector.tensor_copy(x_codes[:], word_table[:].indirect(entries(offs_sb, start, end)))
+        def gather_words(start, tag):
+            x_codes = keep.tile([P, HALF], U32, name=f"x_codes{start}", tag=tag, align_bytes=64)
+            nc.vector.tensor_copy(x_codes[:], word_table[:].indirect(entries(offs_sb, start, start + HALF)))
             return x_codes
 
-        def products(m, h, x_codes, widths):
-            start, end = parts[h]
-            y = keep.tile([P, end - start], F32, name=f"y{m}_{start}", align_bytes=64)
-            for i, width in enumerate(widths):
-                a = sum(widths[:i])
-                acc = psum.tile([P, width], F32, name=f"acc{m}_{start + a}", tag=f"bank{(3 * (m + 2 * h) + i) % 8}")
-                nc.tensor.matmul_mx(
-                    out=acc[:],
-                    lhsT=w_codes[m][:].bitcast(FP8X4),
-                    lhsT_scale=w_bytes[m][:],
-                    rhs=x_codes[:, a : a + width].bitcast(FP8X4),
-                    rhs_scale=x_bytes[h][:, a : a + width],
-                    start=True,
-                    stop=True,
-                )
-                nc.scalar.copy(y[:, a : a + width], acc[:])
-            return y
+        def product(m, a, b):
+            h = a // FIRST
+            acc = psum.tile([P, b - a], F32, name=f"acc{m}_{a}", tag=f"bank{len(passes) % 8}")
+            passes.append((m, a, b))
+            nc.tensor.matmul_mx(
+                out=acc[:],
+                lhsT=w_codes[m][:].bitcast(FP8X4),
+                lhsT_scale=w_bytes[m][:],
+                rhs=x_codes[a // HALF][:, a % HALF : a % HALF + b - a].bitcast(FP8X4),
+                rhs_scale=x_bytes[h][:, a - h * FIRST : b - h * FIRST],
+                start=True,
+                stop=True,
+            )
+            nc.scalar.copy(y[m][:, a:b], acc[:])
 
-        def scale_columns(m, a, b, y_columns):
-            nc.vector.tensor_tensor(scaled[m][:, a:b], scale_tables[m][:].indirect(entries(task_sb, a, b)), y_columns, MULT)
+        def scale_columns(m, a, b):
+            nc.vector.tensor_tensor(scaled[m][:, a:b], scale_tables[m][:].indirect(entries(task_sb, a, b)), y[m][:, a:b], MULT)
 
         nc.vector.memset(byte_table[:].bitcast(I32), 0)
 
@@ -105,11 +102,11 @@ def tile_picked_none_p_kernel(tc, x_words, x_scales, w1, scale, offs, task, out)
             nc.sync.dma_start(scale_tables[m][:], scale[m * P : (m + 1) * P, :])
         place_bytes(1)
 
-        first_codes = gather_words(0, "first_slot")
+        x_codes = [gather_words(0, "first_slot")]
         nc.scalar.copy(w_grouped[0][:, :, PAIR:PACK], w_late[:].rearrange("p j n -> p n j"))
         quantize(0)
         nc.scalar.copy(w_grouped[1][:], w_second[:].rearrange("p j n -> p n j"))
-        second_codes = gather_words(1, "late_slot")
+        x_codes.append(gather_words(HALF, "late_slot"))
         quantize(1)
 
         scaled = [keep.tile([P, S], F32, name=f"scaled{m}", align_bytes=64) for m in blocks]
@@ -117,16 +114,26 @@ def tile_picked_none_p_kernel(tc, x_words, x_scales, w1, scale, offs, task, out)
         def store(m, a, b):
             nc.sync.dma_start(out[m * P : (m + 1) * P, a:b], scaled[m][:, a:b])
 
-        for m in blocks:
-            y = products(m, 0, first_codes, (256, 256, 128))
-            for a, b in ((0, QUARTER), (QUARTER, FIRST)) if m == 0 else ((0, FIRST),):
-                scale_columns(m, a, b, y[:, a:b])
-            store(m, 0, FIRST // 2)
-            store(m, FIRST // 2, FIRST)
-        middle = (FIRST + S) // 2
-        scale_columns(0, FIRST, S, products(0, 1, second_codes, (256, 128))[:])
-        store(0, FIRST, S)
-        y_last = products(1, 1, second_codes, (256, 128))
-        for a, b in ((FIRST, middle), (middle, S)):
-            scale_columns(1, a, b, y_last[:, a - FIRST : b - FIRST])
-            store(1, a, b)
+        y = [keep.tile([P, S], F32, name=f"y{m}", align_bytes=64) for m in blocks]
+        passes = []
+
+        def piece(m, *cuts):
+            for a, b in zip(cuts, cuts[1:]):
+                product(m, a, b)
+            scale_columns(m, cuts[0], cuts[-1])
+
+        piece(0, 0, 128)
+        piece(0, 128, 384)
+        store(0, 0, 384)
+        piece(0, 384, 512, 640)
+        store(0, 384, 640)
+        piece(1, 0, 256)
+        store(1, 0, 256)
+        piece(1, 256, 512, 640)
+        store(1, 256, 640)
+        piece(0, 640, 896, 1024)
+        store(0, 640, 1024)
+        piece(1, 640, 896)
+        store(1, 640, 896)
+        piece(1, 896, 1024)
+        store(1, 896, 1024)

@@ -17,37 +17,36 @@ MULT = mybir.AluOpType.mult
 P = 128
 PACK = 4
 QUADRANT = 32
-LIST = 16
 ROW_STEP = 8
-FIRST = 640
-HALF = S // 2
-QUARTER = S // 4
+LIST = 16
+BANKS = 8
 PAIR = PACK // 2
+HALF = S // 2
+WIDE, NARROW = 256, 128
+FIRST = HALF + NARROW
 
 
 def tile_picked_none_p_kernel(tc, x_words, x_scales, w1, scale, offs, task, out):
     nc = tc.nc
     blocks = range(N // P)
+    byte_parts = ((0, FIRST), (FIRST, S))
     with ExitStack() as ctx:
         lists = ctx.enter_context(tc.tile_pool(name="lists", bufs=1))
         keep = ctx.enter_context(tc.tile_pool(name="keep", bufs=1))
-        shared = ctx.enter_context(tc.tile_pool(name="shared", bufs=1))
         psum = ctx.enter_context(tc.psum_pool(name="psum", bufs=1))
 
         offs_sb = lists.tile([P, S // LIST], U16, name="offs_sb")
         task_sb = lists.tile([P, S // LIST], U16, name="task_sb")
-        byte_table = shared.tile([P, T], U8, name="byte_table", offset=4 * U - T // 2, align_bytes=64)
+        byte_table = keep.tile([P, T], U8, name="byte_table", tag="byte_slot", align_bytes=64)
         word_table = keep.tile([P, T], U32, name="word_table", align_bytes=64)
-        w_early = keep.tile([P, PAIR, P], F32, name="w_early", align_bytes=64)
+        w_early = keep.tile([P, PAIR, P], F32, name="w_early", tag="early_slot", align_bytes=64)
         w_late = keep.tile([P, PAIR, P], F32, name="w_late", tag="late_slot", align_bytes=64)
         w_second = keep.tile([P, PACK, P], F32, name="w_second", align_bytes=64)
         w_grouped = [keep.tile([P, P, PACK], BF16, name=f"w_grouped{m}", align_bytes=64) for m in blocks]
         w_codes = [keep.tile([P, P], U32, name=f"w_codes{m}", align_bytes=64) for m in blocks]
         w_bytes = [keep.tile([P, P], U8, name=f"w_bytes{m}", align_bytes=64) for m in blocks]
-        parts = ((0, FIRST), (FIRST, S))
-        picked_bytes = [keep.tile([P, b - a], U8, name=f"picked_bytes{a}", align_bytes=64) for a, b in parts]
-        x_bytes = [keep.tile([P, b - a], U8, name=f"x_bytes{a}", align_bytes=64) for a, b in parts]
-        scale_tables = []
+        picked_bytes = [keep.tile([P, b - a], U8, name=f"picked_bytes{a}", align_bytes=64) for a, b in byte_parts]
+        x_bytes = [keep.tile([P, b - a], U8, name=f"x_bytes{a}", align_bytes=64) for a, b in byte_parts]
 
         def entries(list_tile, a, b):
             return list_tile[:, a // LIST : b // LIST]
@@ -55,38 +54,25 @@ def tile_picked_none_p_kernel(tc, x_words, x_scales, w1, scale, offs, task, out)
         def quantize(m):
             nc.vector.quantize_mx(out=w_codes[m][:].bitcast(FP8X4), scales=w_bytes[m][:], in_=w_grouped[m][:].rearrange("p n j -> p (n j)"))
 
-        def place_bytes(h):
+        def place_bytes(part):
             for r in range(PACK):
-                nc.sync.dma_start(x_bytes[h][r:P:QUADRANT, :].bitcast(I32), picked_bytes[h][r * ROW_STEP : P : QUADRANT, :].bitcast(I32))
+                nc.sync.dma_start(x_bytes[part][r:P:QUADRANT, :].bitcast(I32), picked_bytes[part][r * ROW_STEP : P : QUADRANT, :].bitcast(I32))
+
+        def load_scale(m, tag):
+            table = keep.tile([P, U], F32, name=f"scale_table{m}", tag=tag, align_bytes=64)
+            nc.sync.dma_start(table[:], scale[m * P : (m + 1) * P, :])
+            return table
 
         def gather_words(start, tag):
-            x_codes = keep.tile([P, HALF], U32, name=f"x_codes{start}", tag=tag, align_bytes=64)
-            nc.vector.tensor_copy(x_codes[:], word_table[:].indirect(entries(offs_sb, start, start + HALF)))
-            return x_codes
-
-        def product(m, a, b):
-            h = a // FIRST
-            acc = psum.tile([P, b - a], F32, name=f"acc{m}_{a}", tag=f"bank{len(passes) % 8}")
-            passes.append((m, a, b))
-            nc.tensor.matmul_mx(
-                out=acc[:],
-                lhsT=w_codes[m][:].bitcast(FP8X4),
-                lhsT_scale=w_bytes[m][:],
-                rhs=x_codes[a // HALF][:, a % HALF : a % HALF + b - a].bitcast(FP8X4),
-                rhs_scale=x_bytes[h][:, a - h * FIRST : b - h * FIRST],
-                start=True,
-                stop=True,
-            )
-            nc.scalar.copy(y[m][:, a:b], acc[:])
-
-        def scale_columns(m, a, b):
-            nc.vector.tensor_tensor(scaled[m][:, a:b], scale_tables[m][:].indirect(entries(task_sb, a, b)), y[m][:, a:b], MULT)
+            codes = keep.tile([P, HALF], U32, name=f"x_codes{start}", tag=tag, align_bytes=64)
+            nc.vector.tensor_copy(codes[:], word_table[:].indirect(entries(offs_sb, start, start + HALF)))
+            return codes
 
         nc.vector.memset(byte_table[:].bitcast(I32), 0)
 
         w_rows = w1.rearrange("(p j) n -> p j n", j=PACK)
-        nc.sync.dma_start(w_early[:], w_rows[:, 0:PAIR, 0:P])
         nc.sync.dma_start(offs_sb[:], offs)
+        nc.sync.dma_start(w_early[:], w_rows[:, 0:PAIR, 0:P])
         nc.sync.dma_start(byte_table[0:P:ROW_STEP, :].bitcast(I32), x_scales[0].bitcast(I32))
         nc.sync.dma_start(word_table[:].bitcast(I32), x_words[0].rearrange("p t r -> p (t r)").bitcast(I32))
         nc.sync.dma_start(w_late[:], w_rows[:, PAIR:PACK, 0:P])
@@ -94,12 +80,10 @@ def tile_picked_none_p_kernel(tc, x_words, x_scales, w1, scale, offs, task, out)
         nc.sync.dma_start(task_sb[:], task)
 
         nc.scalar.copy(w_grouped[0][:, :, 0:PAIR], w_early[:].rearrange("p j n -> p n j"))
-        for h in range(2):
-            nc.vector.tensor_copy(picked_bytes[h][:], byte_table[:].indirect(entries(offs_sb, *parts[h])))
+        for picked, (a, b) in zip(picked_bytes, byte_parts):
+            nc.vector.tensor_copy(picked[:], byte_table[:].indirect(entries(offs_sb, a, b)))
         place_bytes(0)
-        for m in blocks:
-            scale_tables.append(shared.tile([P, U], F32, name=f"scale_table{m}", offset=4 * U * m, align_bytes=64))
-            nc.sync.dma_start(scale_tables[m][:], scale[m * P : (m + 1) * P, :])
+        scale_tables = [load_scale(0, "early_slot"), load_scale(1, "byte_slot")]
         place_bytes(1)
 
         x_codes = [gather_words(0, "first_slot")]
@@ -110,30 +94,44 @@ def tile_picked_none_p_kernel(tc, x_words, x_scales, w1, scale, offs, task, out)
         quantize(1)
 
         scaled = [keep.tile([P, S], F32, name=f"scaled{m}", align_bytes=64) for m in blocks]
-
-        def store(m, a, b):
-            nc.sync.dma_start(out[m * P : (m + 1) * P, a:b], scaled[m][:, a:b])
-
         y = [keep.tile([P, S], F32, name=f"y{m}", align_bytes=64) for m in blocks]
         passes = []
+
+        def product(m, a, b):
+            part = a // FIRST
+            acc = psum.tile([P, b - a], F32, name=f"acc{m}_{a}", tag=f"bank{len(passes) % BANKS}")
+            passes.append((m, a))
+            nc.tensor.matmul_mx(
+                out=acc[:],
+                lhsT=w_codes[m][:].bitcast(FP8X4),
+                lhsT_scale=w_bytes[m][:],
+                rhs=x_codes[a // HALF][:, a % HALF : a % HALF + b - a].bitcast(FP8X4),
+                rhs_scale=x_bytes[part][:, a - part * FIRST : b - part * FIRST],
+                start=True,
+                stop=True,
+            )
+            nc.scalar.copy(y[m][:, a:b], acc[:])
 
         def piece(m, *cuts):
             for a, b in zip(cuts, cuts[1:]):
                 product(m, a, b)
-            scale_columns(m, cuts[0], cuts[-1])
+            a, b = cuts[0], cuts[-1]
+            nc.vector.tensor_tensor(scaled[m][:, a:b], scale_tables[m][:].indirect(entries(task_sb, a, b)), y[m][:, a:b], MULT)
 
-        piece(0, 0, 128)
-        piece(0, 128, 384)
-        store(0, 0, 384)
-        piece(0, 384, 512, 640)
-        store(0, 384, 640)
-        piece(1, 0, 256)
-        store(1, 0, 256)
-        piece(1, 256, 512, 640)
-        store(1, 256, 640)
-        piece(0, 640, 896, 1024)
-        store(0, 640, 1024)
-        piece(1, 640, 896)
-        store(1, 640, 896)
-        piece(1, 896, 1024)
-        store(1, 896, 1024)
+        def store(m, a, b):
+            nc.sync.dma_start(out[m * P : (m + 1) * P, a:b], scaled[m][:, a:b])
+
+        piece(0, 0, NARROW)
+        piece(0, NARROW, NARROW + WIDE)
+        store(0, 0, NARROW + WIDE)
+        piece(0, NARROW + WIDE, HALF, FIRST)
+        store(0, NARROW + WIDE, FIRST)
+        piece(1, 0, WIDE)
+        store(1, 0, WIDE)
+        piece(1, WIDE, HALF, FIRST)
+        store(1, WIDE, FIRST)
+        piece(0, FIRST, S - NARROW, S)
+        store(0, FIRST, S)
+        for a, b in ((FIRST, S - NARROW), (S - NARROW, S)):
+            piece(1, a, b)
+            store(1, a, b)

@@ -17,7 +17,8 @@ MULT = mybir.AluOpType.mult
 P = 128
 PACK = 4
 QUADRANT = 32
-ROW_STEP = 8
+ROWS = K // QUADRANT
+ROW_BASE = P - ROWS
 LIST = 16
 BANKS = 8
 PAIR = PACK // 2
@@ -40,8 +41,8 @@ def tile_picked_none_p_kernel(tc, x_words, x_scales, w1, scale, offs, task, out)
         byte_table = keep.tile([P, T], U8, name="byte_table", tag="byte_slot", align_bytes=64)
         word_table = keep.tile([P, T], U32, name="word_table", align_bytes=64)
         w_early = keep.tile([P, PAIR, P], F32, name="w_early", tag="early_slot", align_bytes=64)
-        w_late = keep.tile([P, PAIR, P], F32, name="w_late", tag="late_slot", align_bytes=64)
-        w_second = keep.tile([P, PACK, P], F32, name="w_second", align_bytes=64)
+        w_late = keep.tile([P, PAIR, N], F32, name="w_late", tag="late_slot", align_bytes=64)
+        w_second = keep.tile([P, PAIR, P], F32, name="w_second", align_bytes=64)
         w_grouped = [keep.tile([P, P, PACK], BF16, name=f"w_grouped{m}", align_bytes=64) for m in blocks]
         w_codes = [keep.tile([P, P], U32, name=f"w_codes{m}", align_bytes=64) for m in blocks]
         w_bytes = [keep.tile([P, P], U8, name=f"w_bytes{m}", align_bytes=64) for m in blocks]
@@ -56,27 +57,29 @@ def tile_picked_none_p_kernel(tc, x_words, x_scales, w1, scale, offs, task, out)
 
         def place_bytes(part):
             for r in range(PACK):
-                nc.sync.dma_start(x_bytes[part][r:P:QUADRANT, :].bitcast(I32), picked_bytes[part][r * ROW_STEP : P : QUADRANT, :].bitcast(I32))
+                nc.sync.dma_start(x_bytes[part][r:P:QUADRANT, :].bitcast(I32), picked_bytes[part][ROW_BASE + r : P : PACK, :].bitcast(I32))
 
         def load_scale(m, tag):
             table = keep.tile([P, U], F32, name=f"scale_table{m}", tag=tag, align_bytes=64)
             nc.sync.dma_start(table[:], scale[m * P : (m + 1) * P, :])
             return table
 
-        def gather_words(start, tag):
-            codes = keep.tile([P, HALF], U32, name=f"x_codes{start}", tag=tag, align_bytes=64)
-            nc.vector.tensor_copy(codes[:], word_table[:].indirect(entries(offs_sb, start, start + HALF)))
+        def gather_words(part, tag):
+            a, b = byte_parts[part]
+            codes = keep.tile([P, b - a], U32, name=f"x_codes{a}", tag=tag, align_bytes=64)
+            nc.vector.tensor_copy(codes[:], word_table[:].indirect(entries(offs_sb, a, b)))
             return codes
 
-        nc.vector.memset(byte_table[:].bitcast(I32), 0)
+        nc.vector.memset(byte_table[0 : P - QUADRANT, :].bitcast(I32), 0)
+        nc.vector.memset(byte_table[P - QUADRANT : ROW_BASE, :].bitcast(I32), 0)
 
         w_rows = w1.rearrange("(p j) n -> p j n", j=PACK)
         nc.sync.dma_start(offs_sb[:], offs)
+        nc.sync.dma_start(byte_table[ROW_BASE:P, :].bitcast(I32), x_scales[0].bitcast(I32))
         nc.sync.dma_start(w_early[:], w_rows[:, 0:PAIR, 0:P])
-        nc.sync.dma_start(byte_table[0:P:ROW_STEP, :].bitcast(I32), x_scales[0].bitcast(I32))
         nc.sync.dma_start(word_table[:].bitcast(I32), x_words[0].rearrange("p t r -> p (t r)").bitcast(I32))
-        nc.sync.dma_start(w_late[:], w_rows[:, PAIR:PACK, 0:P])
-        nc.sync.dma_start(w_second[:], w_rows[:, :, P:N])
+        nc.sync.dma_start(w_late[:], w_rows[:, PAIR:PACK, :])
+        nc.sync.dma_start(w_second[:], w_rows[:, 0:PAIR, P:N])
         nc.sync.dma_start(task_sb[:], task)
 
         nc.scalar.copy(w_grouped[0][:, :, 0:PAIR], w_early[:].rearrange("p j n -> p n j"))
@@ -87,10 +90,11 @@ def tile_picked_none_p_kernel(tc, x_words, x_scales, w1, scale, offs, task, out)
         place_bytes(1)
 
         x_codes = [gather_words(0, "first_slot")]
-        nc.scalar.copy(w_grouped[0][:, :, PAIR:PACK], w_late[:].rearrange("p j n -> p n j"))
+        for m in blocks:
+            nc.scalar.copy(w_grouped[m][:, :, PAIR:PACK], w_late[:, :, m * P : (m + 1) * P].rearrange("p j n -> p n j"))
         quantize(0)
-        nc.scalar.copy(w_grouped[1][:], w_second[:].rearrange("p j n -> p n j"))
-        x_codes.append(gather_words(HALF, "late_slot"))
+        nc.scalar.copy(w_grouped[1][:, :, 0:PAIR], w_second[:].rearrange("p j n -> p n j"))
+        x_codes.append(gather_words(1, "late_slot"))
         quantize(1)
 
         scaled = [keep.tile([P, S], F32, name=f"scaled{m}", align_bytes=64) for m in blocks]
@@ -105,7 +109,7 @@ def tile_picked_none_p_kernel(tc, x_words, x_scales, w1, scale, offs, task, out)
                 out=acc[:],
                 lhsT=w_codes[m][:].bitcast(FP8X4),
                 lhsT_scale=w_bytes[m][:],
-                rhs=x_codes[a // HALF][:, a % HALF : a % HALF + b - a].bitcast(FP8X4),
+                rhs=x_codes[part][:, a - part * FIRST : b - part * FIRST].bitcast(FP8X4),
                 rhs_scale=x_bytes[part][:, a - part * FIRST : b - part * FIRST],
                 start=True,
                 stop=True,
@@ -124,7 +128,7 @@ def tile_picked_none_p_kernel(tc, x_words, x_scales, w1, scale, offs, task, out)
         piece(0, 0, NARROW)
         piece(0, NARROW, NARROW + WIDE)
         store(0, 0, NARROW + WIDE)
-        piece(0, NARROW + WIDE, HALF, FIRST)
+        piece(0, NARROW + WIDE, FIRST)
         store(0, NARROW + WIDE, FIRST)
         piece(1, 0, WIDE)
         store(1, 0, WIDE)

@@ -20,6 +20,7 @@ QUADRANT = 32
 ROWS = K // QUADRANT
 ROW_BASE = P - ROWS
 LIST = 16
+TABLE_BYTES = 4 * U
 BANKS = 8
 PAIR = PACK // 2
 HALF = S // 2
@@ -34,13 +35,14 @@ def tile_picked_none_p_kernel(tc, x_words, x_scales, w1, scale, offs, task, out)
     with ExitStack() as ctx:
         lists = ctx.enter_context(tc.tile_pool(name="lists", bufs=1))
         keep = ctx.enter_context(tc.tile_pool(name="keep", bufs=1))
+        shared = ctx.enter_context(tc.tile_pool(name="shared", bufs=1))
         psum = ctx.enter_context(tc.psum_pool(name="psum", bufs=1))
 
         offs_sb = lists.tile([P, S // LIST], U16, name="offs_sb")
         task_sb = lists.tile([P, S // LIST], U16, name="task_sb")
-        byte_table = keep.tile([P, T], U8, name="byte_table", tag="byte_slot", align_bytes=64)
+        byte_table = shared.tile([P, T], U8, name="byte_table", offset=TABLE_BYTES - T // 2, align_bytes=64)
         word_table = keep.tile([P, T], U32, name="word_table", align_bytes=64)
-        w_early = keep.tile([P, PAIR, P], F32, name="w_early", tag="early_slot", align_bytes=64)
+        w_early = keep.tile([P, PAIR, P], F32, name="w_early", align_bytes=64)
         w_late = keep.tile([P, PAIR, N], F32, name="w_late", tag="late_slot", align_bytes=64)
         w_second = keep.tile([P, PAIR, P], F32, name="w_second", align_bytes=64)
         w_grouped = [keep.tile([P, P, PACK], BF16, name=f"w_grouped{m}", align_bytes=64) for m in blocks]
@@ -59,8 +61,8 @@ def tile_picked_none_p_kernel(tc, x_words, x_scales, w1, scale, offs, task, out)
             for r in range(PACK):
                 nc.sync.dma_start(x_bytes[part][r:P:QUADRANT, :].bitcast(I32), picked_bytes[part][ROW_BASE + r : P : PACK, :].bitcast(I32))
 
-        def load_scale(m, tag):
-            table = keep.tile([P, U], F32, name=f"scale_table{m}", tag=tag, align_bytes=64)
+        def load_scale(m):
+            table = shared.tile([P, U], F32, name=f"scale_table{m}", offset=m * TABLE_BYTES, align_bytes=64)
             nc.sync.dma_start(table[:], scale[m * P : (m + 1) * P, :])
             return table
 
@@ -75,8 +77,8 @@ def tile_picked_none_p_kernel(tc, x_words, x_scales, w1, scale, offs, task, out)
 
         w_rows = w1.rearrange("(p j) n -> p j n", j=PACK)
         nc.sync.dma_start(offs_sb[:], offs)
-        nc.sync.dma_start(byte_table[ROW_BASE:P, :].bitcast(I32), x_scales[0].bitcast(I32))
-        nc.sync.dma_start(w_early[:], w_rows[:, 0:PAIR, 0:P])
+        nc.scalar.dma_start(byte_table[ROW_BASE:P, :].bitcast(I32), x_scales[0].bitcast(I32))
+        nc.scalar.dma_start(w_early[:], w_rows[:, 0:PAIR, 0:P])
         nc.sync.dma_start(word_table[:].bitcast(I32), x_words[0].rearrange("p t r -> p (t r)").bitcast(I32))
         nc.sync.dma_start(w_late[:], w_rows[:, PAIR:PACK, :])
         nc.sync.dma_start(w_second[:], w_rows[:, 0:PAIR, P:N])
@@ -86,7 +88,7 @@ def tile_picked_none_p_kernel(tc, x_words, x_scales, w1, scale, offs, task, out)
         for picked, (a, b) in zip(picked_bytes, byte_parts):
             nc.vector.tensor_copy(picked[:], byte_table[:].indirect(entries(offs_sb, a, b)))
         place_bytes(0)
-        scale_tables = [load_scale(0, "early_slot"), load_scale(1, "byte_slot")]
+        scale_tables = [load_scale(m) for m in blocks]
         place_bytes(1)
 
         x_codes = [gather_words(0, "first_slot")]

@@ -17,57 +17,45 @@ MULT = mybir.AluOpType.mult
 P = 128
 PACK = 4
 QUADRANT = 32
-ROWS = K // QUADRANT
-ROW_BASE = P - ROWS
+ROW_BASE = P - K // QUADRANT
 LIST = 16
-TABLE_BYTES = 4 * U
 BANKS = 8
-PAIR = PACK // 2
-HALF = S // 2
-WIDE, NARROW = 256, 128
-FIRST = HALF + NARROW
+FIRST = 768
 
 
 def tile_picked_none_p_kernel(tc, x_words, x_scales, w1, scale, offs, task, out):
     nc = tc.nc
     blocks = range(N // P)
-    byte_parts = ((0, FIRST), (FIRST, S))
+    word_parts = ((0, FIRST), (FIRST, S))
     with ExitStack() as ctx:
         lists = ctx.enter_context(tc.tile_pool(name="lists", bufs=1))
         keep = ctx.enter_context(tc.tile_pool(name="keep", bufs=1))
-        shared = ctx.enter_context(tc.tile_pool(name="shared", bufs=1))
         psum = ctx.enter_context(tc.psum_pool(name="psum", bufs=1))
 
         offs_sb = lists.tile([P, S // LIST], U16, name="offs_sb")
         task_sb = lists.tile([P, S // LIST], U16, name="task_sb")
-        byte_table = shared.tile([P, T], U8, name="byte_table", offset=TABLE_BYTES - T // 2, align_bytes=64)
+        byte_table = keep.tile([P, T], U8, name="byte_table", align_bytes=64)
         word_table = keep.tile([P, T], U32, name="word_table", align_bytes=64)
-        w_early = keep.tile([P, PAIR, P], F32, name="w_early", align_bytes=64)
-        w_late = keep.tile([P, PAIR, N], F32, name="w_late", tag="late_slot", align_bytes=64)
-        w_second = keep.tile([P, PAIR, P], F32, name="w_second", align_bytes=64)
-        w_grouped = [keep.tile([P, P, PACK], BF16, name=f"w_grouped{m}", align_bytes=64) for m in blocks]
+        w_raw = keep.tile([P, PACK, N], F32, name="w_raw", align_bytes=64)
+        w_grouped = [keep.tile([P, P, PACK], BF16, name=f"w_grouped{m}", tag=f"grouped{m}", align_bytes=64) for m in blocks]
         w_codes = [keep.tile([P, P], U32, name=f"w_codes{m}", align_bytes=64) for m in blocks]
         w_bytes = [keep.tile([P, P], U8, name=f"w_bytes{m}", align_bytes=64) for m in blocks]
-        picked_bytes = [keep.tile([P, b - a], U8, name=f"picked_bytes{a}", align_bytes=64) for a, b in byte_parts]
-        x_bytes = [keep.tile([P, b - a], U8, name=f"x_bytes{a}", align_bytes=64) for a, b in byte_parts]
+        picked_bytes = keep.tile([P, S], U8, name="picked_bytes", align_bytes=64)
+        x_bytes = keep.tile([P, S], U8, name="x_bytes", align_bytes=64)
+        tables = [keep.tile([P, U], F32, name=f"scale_table{m}", align_bytes=64) for m in blocks]
 
         def entries(list_tile, a, b):
             return list_tile[:, a // LIST : b // LIST]
 
         def quantize(m):
+            nc.scalar.copy(
+                w_grouped[m][:].rearrange("p (c i) j -> p c j i", i=PACK),
+                w_raw[:, :, m * P : (m + 1) * P].rearrange("p j (c i) -> p c j i", i=PACK),
+            )
             nc.vector.quantize_mx(out=w_codes[m][:].bitcast(FP8X4), scales=w_bytes[m][:], in_=w_grouped[m][:].rearrange("p n j -> p (n j)"))
 
-        def place_bytes(part):
-            for r in range(PACK):
-                nc.sync.dma_start(x_bytes[part][r:P:QUADRANT, :].bitcast(I32), picked_bytes[part][ROW_BASE + r : P : PACK, :].bitcast(I32))
-
-        def load_scale(m):
-            table = shared.tile([P, U], F32, name=f"scale_table{m}", offset=m * TABLE_BYTES, align_bytes=64)
-            nc.sync.dma_start(table[:], scale[m * P : (m + 1) * P, :])
-            return table
-
         def gather_words(part, tag):
-            a, b = byte_parts[part]
+            a, b = word_parts[part]
             codes = keep.tile([P, b - a], U32, name=f"x_codes{a}", tag=tag, align_bytes=64)
             nc.vector.tensor_copy(codes[:], word_table[:].indirect(entries(offs_sb, a, b)))
             return codes
@@ -75,28 +63,20 @@ def tile_picked_none_p_kernel(tc, x_words, x_scales, w1, scale, offs, task, out)
         nc.vector.memset(byte_table[0 : P - QUADRANT, :].bitcast(I32), 0)
         nc.vector.memset(byte_table[P - QUADRANT : ROW_BASE, :].bitcast(I32), 0)
 
-        w_rows = w1.rearrange("(p j) n -> p j n", j=PACK)
         nc.sync.dma_start(offs_sb[:], offs)
         nc.scalar.dma_start(byte_table[ROW_BASE:P, :].bitcast(I32), x_scales[0].bitcast(I32))
-        nc.scalar.dma_start(w_early[:], w_rows[:, 0:PAIR, 0:P])
-        nc.sync.dma_start(word_table[:].bitcast(I32), x_words[0].rearrange("p t r -> p (t r)").bitcast(I32))
-        nc.sync.dma_start(w_late[:], w_rows[:, PAIR:PACK, :])
-        nc.sync.dma_start(w_second[:], w_rows[:, 0:PAIR, P:N])
+        nc.scalar.dma_start(word_table[:].bitcast(I32), x_words[0].rearrange("p t r -> p (t r)").bitcast(I32))
+        nc.scalar.dma_start(w_raw[:], w1.rearrange("(p j) n -> p j n", j=PACK))
         nc.sync.dma_start(task_sb[:], task)
-
-        nc.scalar.copy(w_grouped[0][:, :, 0:PAIR], w_early[:].rearrange("p j n -> p n j"))
-        for picked, (a, b) in zip(picked_bytes, byte_parts):
-            nc.vector.tensor_copy(picked[:], byte_table[:].indirect(entries(offs_sb, a, b)))
-        place_bytes(0)
-        scale_tables = [load_scale(m) for m in blocks]
-        place_bytes(1)
-
-        x_codes = [gather_words(0, "first_slot")]
         for m in blocks:
-            nc.scalar.copy(w_grouped[m][:, :, PAIR:PACK], w_late[:, :, m * P : (m + 1) * P].rearrange("p j n -> p n j"))
+            nc.scalar.dma_start(tables[m][:], scale[m * P : (m + 1) * P, :])
+
+        nc.vector.tensor_copy(picked_bytes[:], byte_table[:].indirect(offs_sb[:]))
+        for r in range(PACK):
+            nc.sync.dma_start(x_bytes[r:P:QUADRANT, :].bitcast(I32), picked_bytes[ROW_BASE + r : P : PACK, :].bitcast(I32))
+        x_codes = [gather_words(0, "first_slot")]
         quantize(0)
-        nc.scalar.copy(w_grouped[1][:, :, 0:PAIR], w_second[:].rearrange("p j n -> p n j"))
-        x_codes.append(gather_words(1, "late_slot"))
+        x_codes.append(gather_words(1, "grouped0"))
         quantize(1)
 
         scaled = [keep.tile([P, S], F32, name=f"scaled{m}", align_bytes=64) for m in blocks]
@@ -112,7 +92,7 @@ def tile_picked_none_p_kernel(tc, x_words, x_scales, w1, scale, offs, task, out)
                 lhsT=w_codes[m][:].bitcast(FP8X4),
                 lhsT_scale=w_bytes[m][:],
                 rhs=x_codes[part][:, a - part * FIRST : b - part * FIRST].bitcast(FP8X4),
-                rhs_scale=x_bytes[part][:, a - part * FIRST : b - part * FIRST],
+                rhs_scale=x_bytes[:, a:b],
                 start=True,
                 stop=True,
             )
@@ -122,22 +102,11 @@ def tile_picked_none_p_kernel(tc, x_words, x_scales, w1, scale, offs, task, out)
             for a, b in zip(cuts, cuts[1:]):
                 product(m, a, b)
             a, b = cuts[0], cuts[-1]
-            nc.vector.tensor_tensor(scaled[m][:, a:b], scale_tables[m][:].indirect(entries(task_sb, a, b)), y[m][:, a:b], MULT)
-
-        def store(m, a, b):
+            nc.vector.tensor_tensor(scaled[m][:, a:b], tables[m][:].indirect(entries(task_sb, a, b)), y[m][:, a:b], MULT)
             nc.sync.dma_start(out[m * P : (m + 1) * P, a:b], scaled[m][:, a:b])
 
-        piece(0, 0, NARROW)
-        piece(0, NARROW, NARROW + WIDE)
-        store(0, 0, NARROW + WIDE)
-        piece(0, NARROW + WIDE, FIRST)
-        store(0, NARROW + WIDE, FIRST)
-        piece(1, 0, WIDE)
-        store(1, 0, WIDE)
-        piece(1, WIDE, HALF, FIRST)
-        store(1, WIDE, FIRST)
-        piece(0, FIRST, S - NARROW, S)
-        store(0, FIRST, S)
-        for a, b in ((FIRST, S - NARROW), (S - NARROW, S)):
-            piece(1, a, b)
-            store(1, a, b)
+        piece(0, 0, 256)
+        piece(0, 256, 512, 768, 1024)
+        piece(1, 0, 512)
+        piece(1, 512, 768, 896)
+        piece(1, 896, 1024)

@@ -21,28 +21,31 @@ ROW_BASE = P - K // QUADRANT
 LIST = 16
 BANKS = 8
 FIRST = 768
+FIRST_BYTES = 640
 
 
 def tile_picked_none_p_kernel(tc, x_words, x_scales, w1, scale, offs, task, out):
     nc = tc.nc
     blocks = range(N // P)
     word_parts = ((0, FIRST), (FIRST, S))
+    byte_parts = ((0, FIRST_BYTES), (FIRST_BYTES, S))
     with ExitStack() as ctx:
         lists = ctx.enter_context(tc.tile_pool(name="lists", bufs=1))
         keep = ctx.enter_context(tc.tile_pool(name="keep", bufs=1))
+        shared = ctx.enter_context(tc.tile_pool(name="shared", bufs=1))
         psum = ctx.enter_context(tc.psum_pool(name="psum", bufs=1))
 
         offs_sb = lists.tile([P, S // LIST], U16, name="offs_sb")
         task_sb = lists.tile([P, S // LIST], U16, name="task_sb")
-        byte_table = keep.tile([P, T], U8, name="byte_table", align_bytes=64)
+        byte_table = shared.tile([P, T], U8, name="byte_table", offset=4 * U - T // 2, align_bytes=64)
         word_table = keep.tile([P, T], U32, name="word_table", align_bytes=64)
         w_raw = keep.tile([P, PACK, N], F32, name="w_raw", align_bytes=64)
         w_grouped = [keep.tile([P, P, PACK], BF16, name=f"w_grouped{m}", tag=f"grouped{m}", align_bytes=64) for m in blocks]
         w_codes = [keep.tile([P, P], U32, name=f"w_codes{m}", align_bytes=64) for m in blocks]
         w_bytes = [keep.tile([P, P], U8, name=f"w_bytes{m}", align_bytes=64) for m in blocks]
-        picked_bytes = keep.tile([P, S], U8, name="picked_bytes", align_bytes=64)
-        x_bytes = keep.tile([P, S], U8, name="x_bytes", align_bytes=64)
-        tables = [keep.tile([P, U], F32, name=f"scale_table{m}", align_bytes=64) for m in blocks]
+        picked_bytes = [keep.tile([P, b - a], U8, name=f"picked_bytes{a}", align_bytes=64) for a, b in byte_parts]
+        x_bytes = [keep.tile([P, b - a], U8, name=f"x_bytes{a}", align_bytes=64) for a, b in byte_parts]
+        tables = [shared.tile([P, U], F32, name=f"scale_table{m}", offset=m * 4 * U, align_bytes=64) for m in blocks]
 
         def entries(list_tile, a, b):
             return list_tile[:, a // LIST : b // LIST]
@@ -53,6 +56,10 @@ def tile_picked_none_p_kernel(tc, x_words, x_scales, w1, scale, offs, task, out)
                 w_raw[:, :, m * P : (m + 1) * P].rearrange("p j (c i) -> p c j i", i=PACK),
             )
             nc.vector.quantize_mx(out=w_codes[m][:].bitcast(FP8X4), scales=w_bytes[m][:], in_=w_grouped[m][:].rearrange("p n j -> p (n j)"))
+
+        def place_bytes(part):
+            for r in range(PACK):
+                nc.sync.dma_start(x_bytes[part][r:P:QUADRANT, :].bitcast(I32), picked_bytes[part][ROW_BASE + r : P : PACK, :].bitcast(I32))
 
         def gather_words(part, tag):
             a, b = word_parts[part]
@@ -65,15 +72,16 @@ def tile_picked_none_p_kernel(tc, x_words, x_scales, w1, scale, offs, task, out)
 
         nc.sync.dma_start(offs_sb[:], offs)
         nc.scalar.dma_start(byte_table[ROW_BASE:P, :].bitcast(I32), x_scales[0].bitcast(I32))
-        nc.scalar.dma_start(word_table[:].bitcast(I32), x_words[0].rearrange("p t r -> p (t r)").bitcast(I32))
-        nc.scalar.dma_start(w_raw[:], w1.rearrange("(p j) n -> p j n", j=PACK))
+        nc.sync.dma_start(word_table[:].bitcast(I32), x_words[0].rearrange("p t r -> p (t r)").bitcast(I32))
+        nc.sync.dma_start(w_raw[:], w1.rearrange("(p j) n -> p j n", j=PACK))
         nc.sync.dma_start(task_sb[:], task)
-        for m in blocks:
-            nc.scalar.dma_start(tables[m][:], scale[m * P : (m + 1) * P, :])
 
-        nc.vector.tensor_copy(picked_bytes[:], byte_table[:].indirect(offs_sb[:]))
-        for r in range(PACK):
-            nc.sync.dma_start(x_bytes[r:P:QUADRANT, :].bitcast(I32), picked_bytes[ROW_BASE + r : P : PACK, :].bitcast(I32))
+        for picked, (a, b) in zip(picked_bytes, byte_parts):
+            nc.vector.tensor_copy(picked[:], byte_table[:].indirect(entries(offs_sb, a, b)))
+        place_bytes(0)
+        nc.sync.dma_start(tables[0][:], scale[0:P, :])
+        nc.sync.dma_start(tables[1][:], scale[P:N, :])
+        place_bytes(1)
         x_codes = [gather_words(0, "first_slot")]
         quantize(0)
         x_codes.append(gather_words(1, "grouped0"))
@@ -92,7 +100,7 @@ def tile_picked_none_p_kernel(tc, x_words, x_scales, w1, scale, offs, task, out)
                 lhsT=w_codes[m][:].bitcast(FP8X4),
                 lhsT_scale=w_bytes[m][:],
                 rhs=x_codes[part][:, a - part * FIRST : b - part * FIRST].bitcast(FP8X4),
-                rhs_scale=x_bytes[:, a:b],
+                rhs_scale=x_bytes[a // FIRST_BYTES][:, a % FIRST_BYTES : a % FIRST_BYTES + b - a],
                 start=True,
                 stop=True,
             )
@@ -106,7 +114,8 @@ def tile_picked_none_p_kernel(tc, x_words, x_scales, w1, scale, offs, task, out)
             nc.sync.dma_start(out[m * P : (m + 1) * P, a:b], scaled[m][:, a:b])
 
         piece(0, 0, 256)
-        piece(0, 256, 512, 768, 1024)
-        piece(1, 0, 512)
-        piece(1, 512, 768, 896)
+        piece(0, 256, 512, 640)
+        piece(1, 0, 512, 640)
+        piece(0, 640, 768, 1024)
+        piece(1, 640, 768, 896)
         piece(1, 896, 1024)

@@ -20,7 +20,7 @@ QUADRANT = 32
 ROW_BASE = P - K // QUADRANT
 LIST = 16
 BANKS = 8
-FIRST = 768
+FIRST = 640
 FIRST_BYTES = 640
 
 
@@ -39,8 +39,8 @@ def tile_picked_none_p_kernel(tc, x_words, x_scales, w1, scale, offs, task, out)
         task_sb = lists.tile([P, S // LIST], U16, name="task_sb")
         byte_table = shared.tile([P, T], U8, name="byte_table", offset=4 * U - T // 2, align_bytes=64)
         word_table = keep.tile([P, T], U32, name="word_table", align_bytes=64)
-        w_raw = keep.tile([P, PACK, N], F32, name="w_raw", align_bytes=64)
-        w_grouped = [keep.tile([P, P, PACK], BF16, name=f"w_grouped{m}", tag=f"grouped{m}", align_bytes=64) for m in blocks]
+        w_raw = [keep.tile([P, PACK, P], F32, name=f"w_raw{m}", tag=f"slot{m}", align_bytes=64) for m in blocks]
+        w_grouped = [keep.tile([P, P, PACK], BF16, name=f"w_grouped{m}", align_bytes=64) for m in blocks]
         w_codes = [keep.tile([P, P], U32, name=f"w_codes{m}", align_bytes=64) for m in blocks]
         w_bytes = [keep.tile([P, P], U8, name=f"w_bytes{m}", align_bytes=64) for m in blocks]
         picked_bytes = [keep.tile([P, b - a], U8, name=f"picked_bytes{a}", align_bytes=64) for a, b in byte_parts]
@@ -53,7 +53,7 @@ def tile_picked_none_p_kernel(tc, x_words, x_scales, w1, scale, offs, task, out)
         def quantize(m):
             nc.scalar.copy(
                 w_grouped[m][:].rearrange("p (c i) j -> p c j i", i=PACK),
-                w_raw[:, :, m * P : (m + 1) * P].rearrange("p j (c i) -> p c j i", i=PACK),
+                w_raw[m][:].rearrange("p j (c i) -> p c j i", i=PACK),
             )
             nc.vector.quantize_mx(out=w_codes[m][:].bitcast(FP8X4), scales=w_bytes[m][:], in_=w_grouped[m][:].rearrange("p n j -> p (n j)"))
 
@@ -70,10 +70,12 @@ def tile_picked_none_p_kernel(tc, x_words, x_scales, w1, scale, offs, task, out)
         nc.vector.memset(byte_table[0 : P - QUADRANT, :].bitcast(I32), 0)
         nc.vector.memset(byte_table[P - QUADRANT : ROW_BASE, :].bitcast(I32), 0)
 
+        w_rows = w1.rearrange("(p j) n -> p j n", j=PACK)
         nc.sync.dma_start(offs_sb[:], offs)
-        nc.scalar.dma_start(byte_table[ROW_BASE:P, :].bitcast(I32), x_scales[0].bitcast(I32))
+        nc.scalar.dma_start(w_raw[0][:], w_rows[:, :, 0:P])
+        nc.sync.dma_start(byte_table[ROW_BASE:P, :].bitcast(I32), x_scales[0].bitcast(I32))
         nc.sync.dma_start(word_table[:].bitcast(I32), x_words[0].rearrange("p t r -> p (t r)").bitcast(I32))
-        nc.sync.dma_start(w_raw[:], w1.rearrange("(p j) n -> p j n", j=PACK))
+        nc.sync.dma_start(w_raw[1][:], w_rows[:, :, P:N])
         nc.sync.dma_start(task_sb[:], task)
 
         for picked, (a, b) in zip(picked_bytes, byte_parts):
@@ -82,10 +84,10 @@ def tile_picked_none_p_kernel(tc, x_words, x_scales, w1, scale, offs, task, out)
         nc.sync.dma_start(tables[0][:], scale[0:P, :])
         nc.sync.dma_start(tables[1][:], scale[P:N, :])
         place_bytes(1)
-        x_codes = [gather_words(0, "first_slot")]
-        quantize(0)
-        x_codes.append(gather_words(1, "grouped0"))
-        quantize(1)
+        x_codes = []
+        for m in blocks:
+            quantize(m)
+            x_codes.append(gather_words(m, f"slot{m}"))
 
         scaled = [keep.tile([P, S], F32, name=f"scaled{m}", align_bytes=64) for m in blocks]
         y = [keep.tile([P, S], F32, name=f"y{m}", align_bytes=64) for m in blocks]
@@ -116,6 +118,6 @@ def tile_picked_none_p_kernel(tc, x_words, x_scales, w1, scale, offs, task, out)
         piece(0, 0, 256)
         piece(0, 256, 512, 640)
         piece(1, 0, 512, 640)
-        piece(0, 640, 768, 1024)
-        piece(1, 640, 768, 896)
+        piece(0, 640, 896, 1024)
+        piece(1, 640, 896)
         piece(1, 896, 1024)

@@ -72,10 +72,10 @@ def tile_picked_none_p_kernel(tc, x_words, x_scales, w1, scale, offs, task, out)
 
         w_rows = w1.rearrange("(p j) n -> p j n", j=PACK)
         nc.sync.dma_start(offs_sb[:], offs)
-        nc.scalar.dma_start(w_raw[0][:], w_rows[:, :, 0:P])
-        nc.sync.dma_start(byte_table[ROW_BASE:P, :].bitcast(I32), x_scales[0].bitcast(I32))
+        nc.scalar.dma_start(byte_table[ROW_BASE:P, :].bitcast(I32), x_scales[0].bitcast(I32))
         nc.sync.dma_start(word_table[:].bitcast(I32), x_words[0].rearrange("p t r -> p (t r)").bitcast(I32))
-        nc.sync.dma_start(w_raw[1][:], w_rows[:, :, P:N])
+        for m in blocks:
+            nc.sync.dma_start(w_raw[m][:], w_rows[:, :, m * P : (m + 1) * P])
         nc.sync.dma_start(task_sb[:], task)
 
         for picked, (a, b) in zip(picked_bytes, byte_parts):
@@ -84,10 +84,10 @@ def tile_picked_none_p_kernel(tc, x_words, x_scales, w1, scale, offs, task, out)
         nc.sync.dma_start(tables[0][:], scale[0:P, :])
         nc.sync.dma_start(tables[1][:], scale[P:N, :])
         place_bytes(1)
-        x_codes = []
-        for m in blocks:
-            quantize(m)
-            x_codes.append(gather_words(m, f"slot{m}"))
+        x_codes = [gather_words(0, "first_slot")]
+        quantize(0)
+        x_codes.append(gather_words(1, "slot0"))
+        quantize(1)
 
         scaled = [keep.tile([P, S], F32, name=f"scaled{m}", align_bytes=64) for m in blocks]
         y = [keep.tile([P, S], F32, name=f"y{m}", align_bytes=64) for m in blocks]
@@ -115,9 +115,11 @@ def tile_picked_none_p_kernel(tc, x_words, x_scales, w1, scale, offs, task, out)
             nc.vector.tensor_tensor(scaled[m][:, a:b], tables[m][:].indirect(entries(task_sb, a, b)), y[m][:, a:b], MULT)
             nc.sync.dma_start(out[m * P : (m + 1) * P, a:b], scaled[m][:, a:b])
 
-        piece(0, 0, 256)
-        piece(0, 256, 512, 640)
-        piece(1, 0, 512, 640)
+        piece(0, 0, 128)
+        piece(0, 128, 384)
+        piece(0, 384, 640)
+        piece(1, 0, 256)
+        piece(1, 256, 512, 640)
         piece(0, 640, 896, 1024)
         piece(1, 640, 896)
         piece(1, 896, 1024)

@@ -37,7 +37,7 @@ def tile_picked_none_p_kernel(tc, x_words, x_scales, w1, scale, offs, task, out)
 
         offs_sb = lists.tile([P, S // LIST], U16, name="offs_sb")
         task_sb = lists.tile([P, S // LIST], U16, name="task_sb")
-        byte_table = shared.tile([P, T], U8, name="byte_table", offset=4 * U - T // 2, align_bytes=64)
+        byte_tables = [shared.tile([P, T], U8, name=f"byte_table{m}", offset=m * 4 * U, align_bytes=64) for m in blocks]
         word_table = keep.tile([P, T], U32, name="word_table", align_bytes=64)
         w_raw = [keep.tile([P, PACK, P], F32, name=f"w_raw{m}", tag=f"slot{m}", align_bytes=64) for m in blocks]
         w_grouped = [keep.tile([P, P, PACK], BF16, name=f"w_grouped{m}", align_bytes=64) for m in blocks]
@@ -67,19 +67,21 @@ def tile_picked_none_p_kernel(tc, x_words, x_scales, w1, scale, offs, task, out)
             nc.vector.tensor_copy(codes[:], word_table[:].indirect(entries(offs_sb, a, b)))
             return codes
 
-        nc.vector.memset(byte_table[0 : P - QUADRANT, :].bitcast(I32), 0)
-        nc.vector.memset(byte_table[P - QUADRANT : ROW_BASE, :].bitcast(I32), 0)
+        for table in byte_tables:
+            nc.vector.memset(table[0 : P - QUADRANT, :].bitcast(I32), 0)
+            nc.vector.memset(table[P - QUADRANT : ROW_BASE, :].bitcast(I32), 0)
 
         w_rows = w1.rearrange("(p j) n -> p j n", j=PACK)
         nc.sync.dma_start(offs_sb[:], offs)
-        nc.scalar.dma_start(byte_table[ROW_BASE:P, :].bitcast(I32), x_scales[0].bitcast(I32))
+        for table in byte_tables:
+            nc.scalar.dma_start(table[ROW_BASE:P, :].bitcast(I32), x_scales[0].bitcast(I32))
+        nc.sync.dma_start(task_sb[:], task)
         nc.sync.dma_start(word_table[:].bitcast(I32), x_words[0].rearrange("p t r -> p (t r)").bitcast(I32))
         for m in blocks:
             nc.sync.dma_start(w_raw[m][:], w_rows[:, :, m * P : (m + 1) * P])
-        nc.sync.dma_start(task_sb[:], task)
 
-        for picked, (a, b) in zip(picked_bytes, byte_parts):
-            nc.vector.tensor_copy(picked[:], byte_table[:].indirect(entries(offs_sb, a, b)))
+        for picked, table, (a, b) in zip(picked_bytes, byte_tables, byte_parts):
+            nc.vector.tensor_copy(picked[:], table[:].indirect(entries(offs_sb, a, b)))
         place_bytes(0)
         nc.sync.dma_start(tables[0][:], scale[0:P, :])
         nc.sync.dma_start(tables[1][:], scale[P:N, :])
@@ -108,18 +110,18 @@ def tile_picked_none_p_kernel(tc, x_words, x_scales, w1, scale, offs, task, out)
             )
             nc.scalar.copy(y[m][:, a:b], acc[:])
 
+        def store(m, a, b):
+            nc.sync.dma_start(out[m * P : (m + 1) * P, a:b], scaled[m][:, a:b])
+
         def piece(m, *cuts):
             for a, b in zip(cuts, cuts[1:]):
                 product(m, a, b)
             a, b = cuts[0], cuts[-1]
             nc.vector.tensor_tensor(scaled[m][:, a:b], tables[m][:].indirect(entries(task_sb, a, b)), y[m][:, a:b], MULT)
-            nc.sync.dma_start(out[m * P : (m + 1) * P, a:b], scaled[m][:, a:b])
 
         piece(0, 0, 128)
         piece(0, 128, 384)
-        piece(0, 384, 640)
-        piece(1, 0, 256)
-        piece(1, 256, 512, 640)
-        piece(0, 640, 896, 1024)
-        piece(1, 640, 896)
-        piece(1, 896, 1024)
+        store(0, 0, 384)
+        for m, cuts in ((0, (384, 640)), (1, (0, 256)), (1, (256, 512, 640)), (0, (640, 896, 1024)), (1, (640, 896)), (1, (896, 1024))):
+            piece(m, *cuts)
+            store(m, cuts[0], cuts[-1])

@@ -19,16 +19,16 @@ PACK = 4
 QUADRANT = 32
 ROW_BASE = P - K // QUADRANT
 LIST = 16
+TABLE_BYTES = 4 * U
 BANKS = 8
-FIRST = 640
-FIRST_BYTES = 640
+WIDE, NARROW = 256, 128
+FIRST = 2 * WIDE + NARROW
 
 
 def tile_picked_none_p_kernel(tc, x_words, x_scales, w1, scale, offs, task, out):
     nc = tc.nc
     blocks = range(N // P)
-    word_parts = ((0, FIRST), (FIRST, S))
-    byte_parts = ((0, FIRST_BYTES), (FIRST_BYTES, S))
+    parts = ((0, FIRST), (FIRST, S))
     with ExitStack() as ctx:
         lists = ctx.enter_context(tc.tile_pool(name="lists", bufs=1))
         keep = ctx.enter_context(tc.tile_pool(name="keep", bufs=1))
@@ -37,15 +37,17 @@ def tile_picked_none_p_kernel(tc, x_words, x_scales, w1, scale, offs, task, out)
 
         offs_sb = lists.tile([P, S // LIST], U16, name="offs_sb")
         task_sb = lists.tile([P, S // LIST], U16, name="task_sb")
-        byte_tables = [shared.tile([P, T], U8, name=f"byte_table{m}", offset=m * 4 * U, align_bytes=64) for m in blocks]
+        byte_tables = [
+            shared.tile([P, T], U8, name=f"byte_table{i}", offset=i * TABLE_BYTES, align_bytes=64) for i in range(len(parts))
+        ]
         word_table = keep.tile([P, T], U32, name="word_table", align_bytes=64)
         w_raw = [keep.tile([P, PACK, P], F32, name=f"w_raw{m}", tag=f"slot{m}", align_bytes=64) for m in blocks]
         w_grouped = [keep.tile([P, P, PACK], BF16, name=f"w_grouped{m}", align_bytes=64) for m in blocks]
         w_codes = [keep.tile([P, P], U32, name=f"w_codes{m}", align_bytes=64) for m in blocks]
         w_bytes = [keep.tile([P, P], U8, name=f"w_bytes{m}", align_bytes=64) for m in blocks]
-        picked_bytes = [keep.tile([P, b - a], U8, name=f"picked_bytes{a}", align_bytes=64) for a, b in byte_parts]
-        x_bytes = [keep.tile([P, b - a], U8, name=f"x_bytes{a}", align_bytes=64) for a, b in byte_parts]
-        tables = [shared.tile([P, U], F32, name=f"scale_table{m}", offset=m * 4 * U, align_bytes=64) for m in blocks]
+        picked_bytes = [keep.tile([P, b - a], U8, name=f"picked_bytes{a}", align_bytes=64) for a, b in parts]
+        x_bytes = [keep.tile([P, b - a], U8, name=f"x_bytes{a}", align_bytes=64) for a, b in parts]
+        scale_tables = [shared.tile([P, U], F32, name=f"scale_table{m}", offset=m * TABLE_BYTES, align_bytes=64) for m in blocks]
 
         def entries(list_tile, a, b):
             return list_tile[:, a // LIST : b // LIST]
@@ -62,14 +64,13 @@ def tile_picked_none_p_kernel(tc, x_words, x_scales, w1, scale, offs, task, out)
                 nc.sync.dma_start(x_bytes[part][r:P:QUADRANT, :].bitcast(I32), picked_bytes[part][ROW_BASE + r : P : PACK, :].bitcast(I32))
 
         def gather_words(part, tag):
-            a, b = word_parts[part]
+            a, b = parts[part]
             codes = keep.tile([P, b - a], U32, name=f"x_codes{a}", tag=tag, align_bytes=64)
             nc.vector.tensor_copy(codes[:], word_table[:].indirect(entries(offs_sb, a, b)))
             return codes
 
         for table in byte_tables:
-            nc.vector.memset(table[0 : P - QUADRANT, :].bitcast(I32), 0)
-            nc.vector.memset(table[P - QUADRANT : ROW_BASE, :].bitcast(I32), 0)
+            nc.vector.memset(table[0:ROW_BASE, :].bitcast(I32), 0)
 
         w_rows = w1.rearrange("(p j) n -> p j n", j=PACK)
         nc.sync.dma_start(offs_sb[:], offs)
@@ -80,12 +81,13 @@ def tile_picked_none_p_kernel(tc, x_words, x_scales, w1, scale, offs, task, out)
         for m in blocks:
             nc.sync.dma_start(w_raw[m][:], w_rows[:, :, m * P : (m + 1) * P])
 
-        for picked, table, (a, b) in zip(picked_bytes, byte_tables, byte_parts):
+        for picked, table, (a, b) in zip(picked_bytes, byte_tables, parts):
             nc.vector.tensor_copy(picked[:], table[:].indirect(entries(offs_sb, a, b)))
         place_bytes(0)
-        nc.sync.dma_start(tables[0][:], scale[0:P, :])
-        nc.sync.dma_start(tables[1][:], scale[P:N, :])
+        for m in blocks:
+            nc.sync.dma_start(scale_tables[m][:], scale[m * P : (m + 1) * P, :])
         place_bytes(1)
+
         x_codes = [gather_words(0, "first_slot")]
         quantize(0)
         x_codes.append(gather_words(1, "slot0"))
@@ -97,31 +99,40 @@ def tile_picked_none_p_kernel(tc, x_words, x_scales, w1, scale, offs, task, out)
 
         def product(m, a, b):
             part = a // FIRST
+            within = slice(a - part * FIRST, b - part * FIRST)
             acc = psum.tile([P, b - a], F32, name=f"acc{m}_{a}", tag=f"bank{len(passes) % BANKS}")
             passes.append((m, a))
             nc.tensor.matmul_mx(
                 out=acc[:],
                 lhsT=w_codes[m][:].bitcast(FP8X4),
                 lhsT_scale=w_bytes[m][:],
-                rhs=x_codes[part][:, a - part * FIRST : b - part * FIRST].bitcast(FP8X4),
-                rhs_scale=x_bytes[a // FIRST_BYTES][:, a % FIRST_BYTES : a % FIRST_BYTES + b - a],
+                rhs=x_codes[part][:, within].bitcast(FP8X4),
+                rhs_scale=x_bytes[part][:, within],
                 start=True,
                 stop=True,
             )
             nc.scalar.copy(y[m][:, a:b], acc[:])
 
-        def store(m, a, b):
-            nc.sync.dma_start(out[m * P : (m + 1) * P, a:b], scaled[m][:, a:b])
-
         def piece(m, *cuts):
             for a, b in zip(cuts, cuts[1:]):
                 product(m, a, b)
             a, b = cuts[0], cuts[-1]
-            nc.vector.tensor_tensor(scaled[m][:, a:b], tables[m][:].indirect(entries(task_sb, a, b)), y[m][:, a:b], MULT)
+            nc.vector.tensor_tensor(scaled[m][:, a:b], scale_tables[m][:].indirect(entries(task_sb, a, b)), y[m][:, a:b], MULT)
 
-        piece(0, 0, 128)
-        piece(0, 128, 384)
-        store(0, 0, 384)
-        for m, cuts in ((0, (384, 640)), (1, (0, 256)), (1, (256, 512, 640)), (0, (640, 896, 1024)), (1, (640, 896)), (1, (896, 1024))):
-            piece(m, *cuts)
-            store(m, cuts[0], cuts[-1])
+        def store(m, a, b):
+            nc.sync.dma_start(out[m * P : (m + 1) * P, a:b], scaled[m][:, a:b])
+
+        piece(0, 0, NARROW)
+        piece(0, NARROW, NARROW + WIDE)
+        store(0, 0, NARROW + WIDE)
+        piece(0, NARROW + WIDE, FIRST)
+        store(0, NARROW + WIDE, FIRST)
+        piece(1, 0, WIDE)
+        store(1, 0, WIDE)
+        piece(1, WIDE, 2 * WIDE, FIRST)
+        store(1, WIDE, FIRST)
+        piece(0, FIRST, S - NARROW, S)
+        store(0, FIRST, S)
+        for a, b in ((FIRST, S - NARROW), (S - NARROW, S)):
+            piece(1, a, b)
+            store(1, a, b)

@@ -13,126 +13,113 @@ U16 = mybir.dt.uint16
 U8 = mybir.dt.uint8
 FP8X4 = mybir.dt.float8_e4m3fn_x4
 MULT = mybir.AluOpType.mult
+COPY = mybir.ActivationFunctionType.Copy
 
 P = 128
 PACK = 4
 QUADRANT = 32
 ROW_BASE = P - K // QUADRANT
 LIST = 16
-TABLE_BYTES = 4 * U
-BANKS = 8
-WIDE, NARROW = 256, 128
-FIRST = 2 * WIDE + NARROW
 
 
 def tile_picked_none_p_kernel(tc, x_words, x_scales, w1, scale, offs, task, out):
     nc = tc.nc
     blocks = range(N // P)
-    parts = ((0, FIRST), (FIRST, S))
     with ExitStack() as ctx:
         lists = ctx.enter_context(tc.tile_pool(name="lists", bufs=1))
         keep = ctx.enter_context(tc.tile_pool(name="keep", bufs=1))
-        shared = ctx.enter_context(tc.tile_pool(name="shared", bufs=1))
         psum = ctx.enter_context(tc.psum_pool(name="psum", bufs=1))
 
         offs_sb = lists.tile([P, S // LIST], U16, name="offs_sb")
         task_sb = lists.tile([P, S // LIST], U16, name="task_sb")
-        byte_tables = [
-            shared.tile([P, T], U8, name=f"byte_table{i}", offset=i * TABLE_BYTES, align_bytes=64) for i in range(len(parts))
-        ]
+        byte_table = keep.tile([P, T], U8, name="byte_table", tag="late_table", align_bytes=64)
         word_table = keep.tile([P, T], U32, name="word_table", align_bytes=64)
-        w_raw = [keep.tile([P, PACK, P], F32, name=f"w_raw{m}", tag=f"slot{m}", align_bytes=64) for m in blocks]
-        w_grouped = [keep.tile([P, P, PACK], BF16, name=f"w_grouped{m}", align_bytes=64) for m in blocks]
+        w_raw = keep.tile([P, PACK, N], F32, name="w_raw", align_bytes=64)
+        w_grouped = [keep.tile([P, P, PACK], BF16, name=f"w_grouped{m}", tag=f"slot{m}", align_bytes=64) for m in blocks]
         w_codes = [keep.tile([P, P], U32, name=f"w_codes{m}", align_bytes=64) for m in blocks]
         w_bytes = [keep.tile([P, P], U8, name=f"w_bytes{m}", align_bytes=64) for m in blocks]
-        picked_bytes = [keep.tile([P, b - a], U8, name=f"picked_bytes{a}", align_bytes=64) for a, b in parts]
-        x_bytes = [keep.tile([P, b - a], U8, name=f"x_bytes{a}", align_bytes=64) for a, b in parts]
-        scale_tables = [shared.tile([P, U], F32, name=f"scale_table{m}", offset=m * TABLE_BYTES, align_bytes=64) for m in blocks]
+        picked_bytes = keep.tile([P, S], U8, name="picked_bytes", align_bytes=64)
+        x_bytes = keep.tile([P, S], U8, name="x_bytes", align_bytes=64)
+        scaled = [keep.tile([P, S], F32, name=f"scaled{m}", align_bytes=64) for m in blocks]
 
         def entries(list_tile, a, b):
             return list_tile[:, a // LIST : b // LIST]
 
-        def quantize(m):
+        def round_weights(m):
             nc.scalar.copy(
                 w_grouped[m][:].rearrange("p (c i) j -> p c j i", i=PACK),
-                w_raw[m][:].rearrange("p j (c i) -> p c j i", i=PACK),
+                w_raw[:, :, m * P : (m + 1) * P].rearrange("p j (c i) -> p c j i", i=PACK),
             )
+
+        def quantize(m):
             nc.vector.quantize_mx(out=w_codes[m][:].bitcast(FP8X4), scales=w_bytes[m][:], in_=w_grouped[m][:].rearrange("p n j -> p (n j)"))
 
-        def place_bytes(part):
-            for r in range(PACK):
-                nc.sync.dma_start(x_bytes[part][r:P:QUADRANT, :].bitcast(I32), picked_bytes[part][ROW_BASE + r : P : PACK, :].bitcast(I32))
+        def load_table(m, tag):
+            table = keep.tile([P, U], F32, name=f"scale_table{m}", tag=tag, align_bytes=64)
+            nc.sync.dma_start(table[:], scale[m * P : (m + 1) * P, :])
+            return table
 
-        def gather_words(part, tag):
-            a, b = parts[part]
-            codes = keep.tile([P, b - a], U32, name=f"x_codes{a}", tag=tag, align_bytes=64)
-            nc.vector.tensor_copy(codes[:], word_table[:].indirect(entries(offs_sb, a, b)))
-            return codes
+        idle = keep.tile([P, 2], F32, name="idle")
+        nc.gpsimd.memset(idle[:, 0:1], 0.0)
+        nc.scalar.activation(idle[:, 1:2], idle[:, 0:1], COPY)
 
-        for table in byte_tables:
-            nc.vector.memset(table[0:ROW_BASE, :].bitcast(I32), 0)
-
-        w_rows = w1.rearrange("(p j) n -> p j n", j=PACK)
+        nc.vector.memset(byte_table[0:ROW_BASE, :].bitcast(I32), 0)
         nc.sync.dma_start(offs_sb[:], offs)
-        for table in byte_tables:
-            nc.scalar.dma_start(table[ROW_BASE:P, :].bitcast(I32), x_scales[0].bitcast(I32))
+        nc.scalar.dma_start(byte_table[ROW_BASE:P, :].bitcast(I32), x_scales[0].bitcast(I32))
         nc.sync.dma_start(task_sb[:], task)
         nc.sync.dma_start(word_table[:].bitcast(I32), x_words[0].rearrange("p t r -> p (t r)").bitcast(I32))
-        for m in blocks:
-            nc.sync.dma_start(w_raw[m][:], w_rows[:, :, m * P : (m + 1) * P])
+        tables = [load_table(0, "early_table")]
+        nc.sync.dma_start(w_raw[:], w1.rearrange("(p j) n -> p j n", j=PACK))
 
-        for picked, table, (a, b) in zip(picked_bytes, byte_tables, parts):
-            nc.vector.tensor_copy(picked[:], table[:].indirect(entries(offs_sb, a, b)))
-        place_bytes(0)
-        for m in blocks:
-            nc.sync.dma_start(scale_tables[m][:], scale[m * P : (m + 1) * P, :])
-        place_bytes(1)
+        nc.vector.tensor_copy(picked_bytes[:], byte_table[:].indirect(offs_sb[:]))
+        for r in range(PACK):
+            nc.sync.dma_start(x_bytes[r:P:QUADRANT, :].bitcast(I32), picked_bytes[ROW_BASE + r : P : PACK, :].bitcast(I32))
+        tables.append(load_table(1, "late_table"))
 
-        x_codes = [gather_words(0, "first_slot")]
-        quantize(0)
-        x_codes.append(gather_words(1, "slot0"))
-        quantize(1)
+        x_codes = keep.tile([P, S], U32, name="x_codes", align_bytes=64)
+        nc.vector.tensor_copy(x_codes[:], word_table[:].indirect(offs_sb[:]))
 
-        scaled = [keep.tile([P, S], F32, name=f"scaled{m}", align_bytes=64) for m in blocks]
-        y = [keep.tile([P, S], F32, name=f"y{m}", align_bytes=64) for m in blocks]
-        passes = []
+        def on_scalar(m, a, b):
+            picked = keep.tile([P, b - a], F32, name=f"looked{m}_{a}", align_bytes=64)
+            nc.scalar.activation(picked[:], tables[m][:].indirect(entries(task_sb, a, b)), COPY)
+            return picked
 
-        def product(m, a, b):
-            part = a // FIRST
-            within = slice(a - part * FIRST, b - part * FIRST)
-            acc = psum.tile([P, b - a], F32, name=f"acc{m}_{a}", tag=f"bank{len(passes) % BANKS}")
-            passes.append((m, a))
+        def on_vector(m, a, b, tag):
+            picked = keep.tile([P, b - a], F32, name=f"looked{m}_{a}", tag=tag, align_bytes=64)
+            nc.vector.tensor_copy(picked[:], tables[m][:].indirect(entries(task_sb, a, b)))
+            return picked
+
+        def piece(m, a, b, picked):
+            acc = psum.tile([P, b - a], F32, name=f"acc{m}_{a}")
             nc.tensor.matmul_mx(
                 out=acc[:],
                 lhsT=w_codes[m][:].bitcast(FP8X4),
                 lhsT_scale=w_bytes[m][:],
-                rhs=x_codes[part][:, within].bitcast(FP8X4),
-                rhs_scale=x_bytes[part][:, within],
+                rhs=x_codes[:, a:b].bitcast(FP8X4),
+                rhs_scale=x_bytes[:, a:b],
                 start=True,
                 stop=True,
             )
-            nc.scalar.copy(y[m][:, a:b], acc[:])
-
-        def piece(m, *cuts):
-            for a, b in zip(cuts, cuts[1:]):
-                product(m, a, b)
-            a, b = cuts[0], cuts[-1]
-            nc.vector.tensor_tensor(scaled[m][:, a:b], scale_tables[m][:].indirect(entries(task_sb, a, b)), y[m][:, a:b], MULT)
+            nc.vector.tensor_tensor(scaled[m][:, a:b], acc[:], picked, MULT)
 
         def store(m, a, b):
             nc.sync.dma_start(out[m * P : (m + 1) * P, a:b], scaled[m][:, a:b])
 
-        piece(0, 0, NARROW)
-        piece(0, NARROW, NARROW + WIDE)
-        store(0, 0, NARROW + WIDE)
-        piece(0, NARROW + WIDE, FIRST)
-        store(0, NARROW + WIDE, FIRST)
-        piece(1, 0, WIDE)
-        store(1, 0, WIDE)
-        piece(1, WIDE, 2 * WIDE, FIRST)
-        store(1, WIDE, FIRST)
-        piece(0, FIRST, S - NARROW, S)
-        store(0, FIRST, S)
-        for a, b in ((FIRST, S - NARROW), (S - NARROW, S)):
-            piece(1, a, b)
+        head = on_scalar(0, 0, 512)
+        for m in blocks:
+            round_weights(m)
+        third = on_vector(0, 512, 768, "third")
+        quantize(0)
+        fourth = on_vector(0, 768, 1024, "slot0")
+        quantize(1)
+        piece(0, 0, 256, head[:, 0:256])
+        store(0, 0, 256)
+        piece(0, 256, 512, head[:, 256:512])
+        piece(0, 512, 768, third[:])
+        store(0, 256, 768)
+        piece(0, 768, 1024, fourth[:])
+        store(0, 768, 1024)
+        for a, b in ((0, 512), (512, 768), (768, 896), (896, 1024)):
+            picked = on_scalar(1, a, b)
+            piece(1, a, b, picked[:])
             store(1, a, b)

@@ -59,17 +59,13 @@ def tile_picked_none_p_kernel(tc, x_words, x_scales, w1, scale, offs, task, out)
             nc.sync.dma_start(table[:], scale[m * P : (m + 1) * P, :])
             return table
 
-        idle = keep.tile([P, 2], F32, name="idle")
-        nc.gpsimd.memset(idle[:, 0:1], 0.0)
-        nc.scalar.activation(idle[:, 1:2], idle[:, 0:1], COPY)
-
         nc.vector.memset(byte_table[0:ROW_BASE, :].bitcast(I32), 0)
         nc.sync.dma_start(offs_sb[:], offs)
         nc.scalar.dma_start(byte_table[ROW_BASE:P, :].bitcast(I32), x_scales[0].bitcast(I32))
         nc.sync.dma_start(task_sb[:], task)
         nc.sync.dma_start(word_table[:].bitcast(I32), x_words[0].rearrange("p t r -> p (t r)").bitcast(I32))
-        tables = [load_table(0, "early_table")]
         nc.sync.dma_start(w_raw[:], w1.rearrange("(p j) n -> p j n", j=PACK))
+        tables = [load_table(0, "early_table")]
 
         nc.vector.tensor_copy(picked_bytes[:], byte_table[:].indirect(offs_sb[:]))
         for r in range(PACK):
@@ -89,37 +85,25 @@ def tile_picked_none_p_kernel(tc, x_words, x_scales, w1, scale, offs, task, out)
             nc.vector.tensor_copy(picked[:], tables[m][:].indirect(entries(task_sb, a, b)))
             return picked
 
-        def piece(m, a, b, picked):
+        def piece(m, picked, *cuts):
+            a, b = cuts[0], cuts[-1]
             acc = psum.tile([P, b - a], F32, name=f"acc{m}_{a}")
-            nc.tensor.matmul_mx(
-                out=acc[:],
-                lhsT=w_codes[m][:].bitcast(FP8X4),
-                lhsT_scale=w_bytes[m][:],
-                rhs=x_codes[:, a:b].bitcast(FP8X4),
-                rhs_scale=x_bytes[:, a:b],
-                start=True,
-                stop=True,
-            )
-            nc.vector.tensor_tensor(scaled[m][:, a:b], acc[:], picked, MULT)
-
-        def store(m, a, b):
+            for c, d in zip(cuts, cuts[1:]):
+                nc.tensor.matmul_mx(
+                    out=acc[:, c - a : d - a],
+                    lhsT=w_codes[m][:].bitcast(FP8X4),
+                    lhsT_scale=w_bytes[m][:],
+                    rhs=x_codes[:, c:d].bitcast(FP8X4),
+                    rhs_scale=x_bytes[:, c:d],
+                    start=True,
+                    stop=True,
+                )
+            nc.vector.tensor_tensor(scaled[m][:, a:b], acc[:], picked[:], MULT)
             nc.sync.dma_start(out[m * P : (m + 1) * P, a:b], scaled[m][:, a:b])
 
-        head = on_scalar(0, 0, 512)
         for m in blocks:
             round_weights(m)
-        third = on_vector(0, 512, 768, "third")
-        quantize(0)
-        fourth = on_vector(0, 768, 1024, "slot0")
-        quantize(1)
-        piece(0, 0, 256, head[:, 0:256])
-        store(0, 0, 256)
-        piece(0, 256, 512, head[:, 256:512])
-        piece(0, 512, 768, third[:])
-        store(0, 256, 768)
-        piece(0, 768, 1024, fourth[:])
-        store(0, 768, 1024)
-        for a, b in ((0, 512), (512, 768), (768, 896), (896, 1024)):
-            picked = on_scalar(1, a, b)
-            piece(1, a, b, picked[:])
-            store(1, a, b)
+            quantize(m)
+        piece(0, on_vector(0, 0, 256, "first"), 0, 256)
+        for m, cuts in ((0, (256, 512)), (0, (512, 1024)), (1, (0, 512)), (1, (512, 768, 896)), (1, (896, 1024))):
+            piece(m, on_scalar(m, cuts[0], cuts[-1]), *cuts)

@@ -34,13 +34,12 @@ def tile_picked_none_p_kernel(tc, x_words, x_scales, w1, scale, offs, task, out)
         task_sb = lists.tile([P, S // LIST], U16, name="task_sb")
         byte_table = keep.tile([P, T], U8, name="byte_table", tag="late_table", align_bytes=64)
         word_table = keep.tile([P, T], U32, name="word_table", align_bytes=64)
-        w_raw = keep.tile([P, PACK, N], F32, name="w_raw", align_bytes=64)
+        w_raw = keep.tile([P, PACK, N], F32, name="w_raw", tag="raw", align_bytes=64)
         w_grouped = [keep.tile([P, P, PACK], BF16, name=f"w_grouped{m}", tag=f"slot{m}", align_bytes=64) for m in blocks]
         w_codes = [keep.tile([P, P], U32, name=f"w_codes{m}", align_bytes=64) for m in blocks]
         w_bytes = [keep.tile([P, P], U8, name=f"w_bytes{m}", align_bytes=64) for m in blocks]
         picked_bytes = keep.tile([P, S], U8, name="picked_bytes", align_bytes=64)
         x_bytes = keep.tile([P, S], U8, name="x_bytes", align_bytes=64)
-        scaled = [keep.tile([P, S], F32, name=f"scaled{m}", align_bytes=64) for m in blocks]
 
         def entries(list_tile, a, b):
             return list_tile[:, a // LIST : b // LIST]
@@ -75,17 +74,10 @@ def tile_picked_none_p_kernel(tc, x_words, x_scales, w1, scale, offs, task, out)
         x_codes = keep.tile([P, S], U32, name="x_codes", align_bytes=64)
         nc.vector.tensor_copy(x_codes[:], word_table[:].indirect(offs_sb[:]))
 
-        def on_scalar(m, a, b):
-            picked = keep.tile([P, b - a], F32, name=f"looked{m}_{a}", align_bytes=64)
-            nc.scalar.activation(picked[:], tables[m][:].indirect(entries(task_sb, a, b)), COPY)
-            return picked
+        def on_scalar(picked, m, a, b):
+            nc.scalar.activation(picked, tables[m][:].indirect(entries(task_sb, a, b)), COPY)
 
-        def on_vector(m, a, b, tag):
-            picked = keep.tile([P, b - a], F32, name=f"looked{m}_{a}", tag=tag, align_bytes=64)
-            nc.vector.tensor_copy(picked[:], tables[m][:].indirect(entries(task_sb, a, b)))
-            return picked
-
-        def piece(m, picked, *cuts):
+        def product(m, *cuts):
             a, b = cuts[0], cuts[-1]
             acc = psum.tile([P, b - a], F32, name=f"acc{m}_{a}")
             for c, d in zip(cuts, cuts[1:]):
@@ -98,12 +90,33 @@ def tile_picked_none_p_kernel(tc, x_words, x_scales, w1, scale, offs, task, out)
                     start=True,
                     stop=True,
                 )
-            nc.vector.tensor_tensor(scaled[m][:, a:b], acc[:], picked[:], MULT)
-            nc.sync.dma_start(out[m * P : (m + 1) * P, a:b], scaled[m][:, a:b])
+            return acc
+
+        def piece(m, picked, *cuts):
+            a, b = cuts[0], cuts[-1]
+            scaled = keep.tile([P, b - a], F32, name=f"scaled{m}_{a}", align_bytes=64)
+            nc.vector.tensor_tensor(scaled[:], product(m, *cuts)[:], picked, MULT)
+            nc.sync.dma_start(out[m * P : (m + 1) * P, a:b], scaled[:])
 
         for m in blocks:
             round_weights(m)
             quantize(m)
-        piece(0, on_vector(0, 0, 256, "first"), 0, 256)
-        for m, cuts in ((0, (256, 512)), (0, (512, 1024)), (1, (0, 512)), (1, (512, 768, 896)), (1, (896, 1024))):
-            piece(m, on_scalar(m, cuts[0], cuts[-1]), *cuts)
+        first = keep.tile([P, 384], F32, name="first", tag="raw", align_bytes=64)
+        nc.vector.tensor_copy(first[:], tables[0][:].indirect(entries(task_sb, 0, 384)))
+        second = keep.tile([P, 256], F32, name="second", tag="second", align_bytes=64)
+        on_scalar(second[:], 0, 384, 640)
+        third = keep.tile([P, 384], F32, name="third", tag="third", align_bytes=64)
+        on_scalar(third[:], 0, 640, 1024)
+        piece(0, first[:, 0:128], 0, 128)
+        y = keep.tile([P, 384], F32, name="y", align_bytes=64)
+        nc.scalar.copy(y[:], product(1, 0, 128, 384)[:])
+        piece(0, first[:, 128:384], 128, 384)
+        piece(0, second[:], 384, 640)
+        piece(0, third[:], 640, 768, 1024)
+        fused = keep.tile([P, 384], F32, name="fused", tag="third", align_bytes=64)
+        nc.vector.tensor_tensor(fused[:], tables[1][:].indirect(entries(task_sb, 0, 384)), y[:], MULT)
+        nc.sync.dma_start(out[P:N, 0:384], fused[:])
+        last = keep.tile([P, 640], F32, name="last", tag="raw", align_bytes=64)
+        for a, b in ((384, 896), (896, 1024)):
+            on_scalar(last[:, a - 384 : b - 384], 1, a, b)
+            piece(1, last[:, a - 384 : b - 384], a, b)

@@ -20,6 +20,7 @@ PACK = 4
 QUADRANT = 32
 ROW_BASE = P - K // QUADRANT
 LIST = 16
+WIDE = 256
 
 
 def tile_picked_none_p_kernel(tc, x_words, x_scales, w1, scale, offs, task, out):
@@ -74,9 +75,6 @@ def tile_picked_none_p_kernel(tc, x_words, x_scales, w1, scale, offs, task, out)
         x_codes = keep.tile([P, S], U32, name="x_codes", align_bytes=64)
         nc.vector.tensor_copy(x_codes[:], word_table[:].indirect(offs_sb[:]))
 
-        def on_scalar(picked, m, a, b):
-            nc.scalar.activation(picked, tables[m][:].indirect(entries(task_sb, a, b)), COPY)
-
         def product(m, *cuts):
             a, b = cuts[0], cuts[-1]
             acc = psum.tile([P, b - a], F32, name=f"acc{m}_{a}")
@@ -92,31 +90,41 @@ def tile_picked_none_p_kernel(tc, x_words, x_scales, w1, scale, offs, task, out)
                 )
             return acc
 
-        def piece(m, picked, *cuts):
-            a, b = cuts[0], cuts[-1]
-            scaled = keep.tile([P, b - a], F32, name=f"scaled{m}_{a}", align_bytes=64)
-            nc.vector.tensor_tensor(scaled[:], product(m, *cuts)[:], picked, MULT)
-            nc.sync.dma_start(out[m * P : (m + 1) * P, a:b], scaled[:])
+        def store(m, a, scaled):
+            nc.sync.dma_start(out[m * P : (m + 1) * P, a : a + WIDE], scaled[:])
+
+        def wide_tile(name, tag):
+            return keep.tile([P, WIDE], F32, name=name, tag=tag, align_bytes=64)
+
+        def table_columns(m, a):
+            return tables[m][:].indirect(entries(task_sb, a, a + WIDE))
+
+        def look_up(m, a, tag):
+            looked = wide_tile(f"looked{m}_{a}", tag)
+            nc.scalar.activation(looked[:], table_columns(m, a), COPY)
+            return looked
+
+        def leave_psum(m, a):
+            y = wide_tile(f"y{m}_{a}", f"y{m}_{a}")
+            nc.scalar.copy(y[:], product(m, a, a + WIDE)[:])
+            return y
+
+        def multiply(m, a, first, second):
+            scaled = wide_tile(f"scaled{m}_{a}", f"scaled{m}_{a}")
+            nc.vector.tensor_tensor(scaled[:], first, second[:], MULT)
+            store(m, a, scaled)
 
         for m in blocks:
             round_weights(m)
             quantize(m)
-        first = keep.tile([P, 384], F32, name="first", tag="raw", align_bytes=64)
-        nc.vector.tensor_copy(first[:], tables[0][:].indirect(entries(task_sb, 0, 384)))
-        second = keep.tile([P, 256], F32, name="second", tag="second", align_bytes=64)
-        on_scalar(second[:], 0, 384, 640)
-        third = keep.tile([P, 384], F32, name="third", tag="third", align_bytes=64)
-        on_scalar(third[:], 0, 640, 1024)
-        piece(0, first[:, 0:128], 0, 128)
-        y = keep.tile([P, 384], F32, name="y", align_bytes=64)
-        nc.scalar.copy(y[:], product(1, 0, 128, 384)[:])
-        piece(0, first[:, 128:384], 128, 384)
-        piece(0, second[:], 384, 640)
-        piece(0, third[:], 640, 768, 1024)
-        fused = keep.tile([P, 384], F32, name="fused", tag="third", align_bytes=64)
-        nc.vector.tensor_tensor(fused[:], tables[1][:].indirect(entries(task_sb, 0, 384)), y[:], MULT)
-        nc.sync.dma_start(out[P:N, 0:384], fused[:])
-        last = keep.tile([P, 640], F32, name="last", tag="raw", align_bytes=64)
-        for a, b in ((384, 896), (896, 1024)):
-            on_scalar(last[:, a - 384 : b - 384], 1, a, b)
-            piece(1, last[:, a - 384 : b - 384], a, b)
+        looked = [look_up(0, 0, "first"), wide_tile("second", "raw")]
+        nc.vector.tensor_copy(looked[1][:], table_columns(0, WIDE))
+        looked.extend(look_up(0, a, f"looked{a}") for a in (2 * WIDE, 3 * WIDE))
+        for i in range(3):
+            multiply(0, i * WIDE, product(0, i * WIDE, (i + 1) * WIDE)[:], looked[i])
+        copied = [leave_psum(1, a) for a in (0, WIDE)]
+        multiply(0, 3 * WIDE, product(0, 3 * WIDE, S)[:], looked[3])
+        for i, y in enumerate(copied):
+            multiply(1, i * WIDE, table_columns(1, i * WIDE), y)
+        for a in (2 * WIDE, 3 * WIDE):
+            multiply(1, a, product(1, a, a + WIDE)[:], look_up(1, a, f"late{a}"))

@@ -25,7 +25,6 @@ WIDE = 256
 
 def tile_picked_none_p_kernel(tc, x_words, x_scales, w1, scale, offs, task, out):
     nc = tc.nc
-    blocks = range(N // P)
     with ExitStack() as ctx:
         lists = ctx.enter_context(tc.tile_pool(name="lists", bufs=1))
         keep = ctx.enter_context(tc.tile_pool(name="keep", bufs=1))
@@ -36,23 +35,14 @@ def tile_picked_none_p_kernel(tc, x_words, x_scales, w1, scale, offs, task, out)
         byte_table = keep.tile([P, T], U8, name="byte_table", tag="late_table", align_bytes=64)
         word_table = keep.tile([P, T], U32, name="word_table", align_bytes=64)
         w_raw = keep.tile([P, PACK, N], F32, name="w_raw", tag="raw", align_bytes=64)
-        w_grouped = [keep.tile([P, P, PACK], BF16, name=f"w_grouped{m}", tag=f"slot{m}", align_bytes=64) for m in blocks]
-        w_codes = [keep.tile([P, P], U32, name=f"w_codes{m}", align_bytes=64) for m in blocks]
-        w_bytes = [keep.tile([P, P], U8, name=f"w_bytes{m}", align_bytes=64) for m in blocks]
+        w_grouped = keep.tile([P, N, PACK], BF16, name="w_grouped", align_bytes=64)
+        w_codes = keep.tile([P, N], U32, name="w_codes", align_bytes=64)
+        w_bytes = keep.tile([P, N], U8, name="w_bytes", align_bytes=64)
         picked_bytes = keep.tile([P, S], U8, name="picked_bytes", align_bytes=64)
         x_bytes = keep.tile([P, S], U8, name="x_bytes", align_bytes=64)
 
         def entries(list_tile, a, b):
             return list_tile[:, a // LIST : b // LIST]
-
-        def round_weights(m):
-            nc.scalar.copy(
-                w_grouped[m][:].rearrange("p (c i) j -> p c j i", i=PACK),
-                w_raw[:, :, m * P : (m + 1) * P].rearrange("p j (c i) -> p c j i", i=PACK),
-            )
-
-        def quantize(m):
-            nc.vector.quantize_mx(out=w_codes[m][:].bitcast(FP8X4), scales=w_bytes[m][:], in_=w_grouped[m][:].rearrange("p n j -> p (n j)"))
 
         def load_table(m, tag):
             table = keep.tile([P, U], F32, name=f"scale_table{m}", tag=tag, align_bytes=64)
@@ -62,9 +52,9 @@ def tile_picked_none_p_kernel(tc, x_words, x_scales, w1, scale, offs, task, out)
         nc.vector.memset(byte_table[0:ROW_BASE, :].bitcast(I32), 0)
         nc.sync.dma_start(offs_sb[:], offs)
         nc.scalar.dma_start(byte_table[ROW_BASE:P, :].bitcast(I32), x_scales[0].bitcast(I32))
-        nc.sync.dma_start(task_sb[:], task)
         nc.sync.dma_start(word_table[:].bitcast(I32), x_words[0].rearrange("p t r -> p (t r)").bitcast(I32))
         nc.sync.dma_start(w_raw[:], w1.rearrange("(p j) n -> p j n", j=PACK))
+        nc.sync.dma_start(task_sb[:], task)
         tables = [load_table(0, "early_table")]
 
         nc.vector.tensor_copy(picked_bytes[:], byte_table[:].indirect(offs_sb[:]))
@@ -81,8 +71,8 @@ def tile_picked_none_p_kernel(tc, x_words, x_scales, w1, scale, offs, task, out)
             for c, d in zip(cuts, cuts[1:]):
                 nc.tensor.matmul_mx(
                     out=acc[:, c - a : d - a],
-                    lhsT=w_codes[m][:].bitcast(FP8X4),
-                    lhsT_scale=w_bytes[m][:],
+                    lhsT=w_codes[:, m * P : (m + 1) * P].bitcast(FP8X4),
+                    lhsT_scale=w_bytes[:, m * P : (m + 1) * P],
                     rhs=x_codes[:, c:d].bitcast(FP8X4),
                     rhs_scale=x_bytes[:, c:d],
                     start=True,
@@ -90,41 +80,38 @@ def tile_picked_none_p_kernel(tc, x_words, x_scales, w1, scale, offs, task, out)
                 )
             return acc
 
-        def store(m, a, scaled):
-            nc.sync.dma_start(out[m * P : (m + 1) * P, a : a + WIDE], scaled[:])
+        def new_tile(name, a, b, tag):
+            return keep.tile([P, b - a], F32, name=f"{name}_{a}", tag=tag, align_bytes=64)
 
-        def wide_tile(name, tag):
-            return keep.tile([P, WIDE], F32, name=name, tag=tag, align_bytes=64)
+        def table_columns(m, a, b):
+            return tables[m][:].indirect(entries(task_sb, a, b))
 
-        def table_columns(m, a):
-            return tables[m][:].indirect(entries(task_sb, a, a + WIDE))
-
-        def look_up(m, a, tag):
-            looked = wide_tile(f"looked{m}_{a}", tag)
-            nc.scalar.activation(looked[:], table_columns(m, a), COPY)
+        def look_up(m, a, b):
+            looked = new_tile(f"looked{m}", a, b, f"looked{m}_{a}")
+            nc.scalar.activation(looked[:], table_columns(m, a, b), COPY)
             return looked
 
-        def leave_psum(m, a):
-            y = wide_tile(f"y{m}_{a}", f"y{m}_{a}")
-            nc.scalar.copy(y[:], product(m, a, a + WIDE)[:])
-            return y
-
-        def multiply(m, a, first, second):
-            scaled = wide_tile(f"scaled{m}_{a}", f"scaled{m}_{a}")
+        def multiply(m, a, b, first, second):
+            scaled = new_tile(f"scaled{m}", a, b, f"scaled{m}_{a}")
             nc.vector.tensor_tensor(scaled[:], first, second[:], MULT)
-            store(m, a, scaled)
+            queue = nc.scalar if (m, b) == (1, S) else nc.sync
+            queue.dma_start(out[m * P : (m + 1) * P, a:b], scaled[:])
 
-        for m in blocks:
-            round_weights(m)
-            quantize(m)
-        looked = [look_up(0, 0, "first"), wide_tile("second", "raw")]
-        nc.vector.tensor_copy(looked[1][:], table_columns(0, WIDE))
-        looked.extend(look_up(0, a, f"looked{a}") for a in (2 * WIDE, 3 * WIDE))
-        for i in range(3):
-            multiply(0, i * WIDE, product(0, i * WIDE, (i + 1) * WIDE)[:], looked[i])
-        copied = [leave_psum(1, a) for a in (0, WIDE)]
-        multiply(0, 3 * WIDE, product(0, 3 * WIDE, S)[:], looked[3])
-        for i, y in enumerate(copied):
-            multiply(1, i * WIDE, table_columns(1, i * WIDE), y)
-        for a in (2 * WIDE, 3 * WIDE):
-            multiply(1, a, product(1, a, a + WIDE)[:], look_up(1, a, f"late{a}"))
+        nc.scalar.copy(
+            w_grouped[:].rearrange("p (c i) j -> p c j i", i=PACK),
+            w_raw[:].rearrange("p j (c i) -> p c j i", i=PACK),
+        )
+        nc.vector.quantize_mx(out=w_codes[:].bitcast(FP8X4), scales=w_bytes[:], in_=w_grouped[:].rearrange("p n j -> p (n j)"))
+        first = look_up(0, 0, 256)
+        second = new_tile("looked0", 256, 640, "raw")
+        nc.vector.tensor_copy(second[:], table_columns(0, 256, 640))
+        third = look_up(0, 640, 1024)
+        multiply(0, 0, 256, product(0, 0, 256)[:], first)
+        y = new_tile("y", 0, 256, "y")
+        nc.scalar.copy(y[:], product(1, 0, 256)[:])
+        multiply(0, 256, 640, product(0, 256, 512, 640)[:], second)
+        multiply(0, 640, 1024, product(0, 640, 896, 1024)[:], third)
+        multiply(1, 0, 256, table_columns(1, 0, 256), y)
+        for cuts in ((256, 512, 640), (640, 896), (896, 1024)):
+            a, b = cuts[0], cuts[-1]
+            multiply(1, a, b, product(1, *cuts)[:], look_up(1, a, b))

@@ -97,11 +97,15 @@ def tile_picked_none_p_kernel(tc, x_words, x_scales, w1, scale, offs, task, out)
             queue = nc.scalar if (m, b) == (1, S) else nc.sync
             queue.dma_start(out[m * P : (m + 1) * P, a:b], scaled[:])
 
-        nc.scalar.copy(
-            w_grouped[:].rearrange("p (c i) j -> p c j i", i=PACK),
-            w_raw[:].rearrange("p j (c i) -> p c j i", i=PACK),
-        )
-        nc.vector.quantize_mx(out=w_codes[:].bitcast(FP8X4), scales=w_bytes[:], in_=w_grouped[:].rearrange("p n j -> p (n j)"))
+        for m in range(N // P):
+            cols = slice(m * P, (m + 1) * P)
+            nc.scalar.copy(
+                w_grouped[:, cols, :].rearrange("p (c i) j -> p c j i", i=PACK),
+                w_raw[:, :, cols].rearrange("p j (c i) -> p c j i", i=PACK),
+            )
+            nc.vector.quantize_mx(
+                out=w_codes[:, cols].bitcast(FP8X4), scales=w_bytes[:, cols], in_=w_grouped[:, cols, :].rearrange("p n j -> p (n j)")
+            )
         first = look_up(0, 0, 256)
         second = new_tile("looked0", 256, 640, "raw")
         nc.vector.tensor_copy(second[:], table_columns(0, 256, 640))

@@ -20,7 +20,7 @@ PACK = 4
 QUADRANT = 32
 ROW_BASE = P - K // QUADRANT
 LIST = 16
-WIDE = 256
+ALIGN = 256
 
 
 def tile_picked_none_p_kernel(tc, x_words, x_scales, w1, scale, offs, task, out):
@@ -32,20 +32,20 @@ def tile_picked_none_p_kernel(tc, x_words, x_scales, w1, scale, offs, task, out)
 
         offs_sb = lists.tile([P, S // LIST], U16, name="offs_sb")
         task_sb = lists.tile([P, S // LIST], U16, name="task_sb")
-        byte_table = keep.tile([P, T], U8, name="byte_table", tag="late_table", align_bytes=64)
-        word_table = keep.tile([P, T], U32, name="word_table", align_bytes=64)
-        w_raw = keep.tile([P, PACK, N], F32, name="w_raw", tag="raw", align_bytes=64)
-        w_grouped = keep.tile([P, N, PACK], BF16, name="w_grouped", align_bytes=64)
-        w_codes = keep.tile([P, N], U32, name="w_codes", align_bytes=64)
-        w_bytes = keep.tile([P, N], U8, name="w_bytes", align_bytes=64)
-        picked_bytes = keep.tile([P, S], U8, name="picked_bytes", align_bytes=64)
-        x_bytes = keep.tile([P, S], U8, name="x_bytes", align_bytes=64)
+        byte_table = keep.tile([P, T], U8, name="byte_table", tag="late_table", align_bytes=ALIGN)
+        word_table = keep.tile([P, T], U32, name="word_table", align_bytes=ALIGN)
+        w_raw = keep.tile([P, PACK, N], F32, name="w_raw", tag="raw", align_bytes=ALIGN)
+        w_grouped = keep.tile([P, N, PACK], BF16, name="w_grouped", align_bytes=ALIGN)
+        w_codes = keep.tile([P, N], U32, name="w_codes", align_bytes=ALIGN)
+        w_bytes = keep.tile([P, N], U8, name="w_bytes", align_bytes=ALIGN)
+        picked_bytes = keep.tile([P, S], U8, name="picked_bytes", align_bytes=ALIGN)
+        x_bytes = keep.tile([P, S], U8, name="x_bytes", align_bytes=ALIGN)
 
         def entries(list_tile, a, b):
             return list_tile[:, a // LIST : b // LIST]
 
         def load_table(m, tag):
-            table = keep.tile([P, U], F32, name=f"scale_table{m}", tag=tag, align_bytes=64)
+            table = keep.tile([P, U], F32, name=f"scale_table{m}", tag=tag, align_bytes=ALIGN)
             nc.sync.dma_start(table[:], scale[m * P : (m + 1) * P, :])
             return table
 
@@ -62,7 +62,7 @@ def tile_picked_none_p_kernel(tc, x_words, x_scales, w1, scale, offs, task, out)
             nc.sync.dma_start(x_bytes[r:P:QUADRANT, :].bitcast(I32), picked_bytes[ROW_BASE + r : P : PACK, :].bitcast(I32))
         tables.append(load_table(1, "late_table"))
 
-        x_codes = keep.tile([P, S], U32, name="x_codes", align_bytes=64)
+        x_codes = keep.tile([P, S], U32, name="x_codes", align_bytes=ALIGN)
         nc.vector.tensor_copy(x_codes[:], word_table[:].indirect(offs_sb[:]))
 
         def product(m, *cuts):
@@ -81,7 +81,7 @@ def tile_picked_none_p_kernel(tc, x_words, x_scales, w1, scale, offs, task, out)
             return acc
 
         def new_tile(name, a, b, tag):
-            return keep.tile([P, b - a], F32, name=f"{name}_{a}", tag=tag, align_bytes=64)
+            return keep.tile([P, b - a], F32, name=f"{name}_{a}", tag=tag, align_bytes=ALIGN)
 
         def table_columns(m, a, b):
             return tables[m][:].indirect(entries(task_sb, a, b))

@@ -13,6 +13,7 @@ U16 = mybir.dt.uint16
 U8 = mybir.dt.uint8
 FP8X4 = mybir.dt.float8_e4m3fn_x4
 MULT = mybir.AluOpType.mult
+ADD = mybir.AluOpType.add
 COPY = mybir.ActivationFunctionType.Copy
 
 P = 128
@@ -99,10 +100,13 @@ def tile_picked_none_p_kernel(tc, x_words, x_scales, w1, scale, offs, task, out)
 
         for m in range(N // P):
             cols = slice(m * P, (m + 1) * P)
-            nc.scalar.copy(
-                w_grouped[:, cols, :].rearrange("p (c i) j -> p c j i", i=PACK),
-                w_raw[:, :, cols].rearrange("p j (c i) -> p c j i", i=PACK),
-            )
+            if m == 0:
+                nc.scalar.copy(
+                    w_grouped[:, cols, :].rearrange("p (c i) j -> p c j i", i=PACK),
+                    w_raw[:, :, cols].rearrange("p j (c i) -> p c j i", i=PACK),
+                )
+            else:
+                nc.gpsimd.tensor_scalar(w_grouped[:, cols, :], w_raw[:, :, cols].rearrange("p j n -> p n j"), 1.0, 0.0, MULT, ADD)
             nc.vector.quantize_mx(
                 out=w_codes[:, cols].bitcast(FP8X4), scales=w_bytes[:, cols], in_=w_grouped[:, cols, :].rearrange("p n j -> p (n j)")
             )

@@ -22,6 +22,7 @@ QUADRANT = 32
 ROW_BASE = P - K // QUADRANT
 LIST = 16
 ALIGN = 256
+EARLY = 896
 
 
 def tile_picked_none_p_kernel(tc, x_words, x_scales, w1, scale, offs, task, out):
@@ -36,7 +37,7 @@ def tile_picked_none_p_kernel(tc, x_words, x_scales, w1, scale, offs, task, out)
         byte_table = keep.tile([P, T], U8, name="byte_table", tag="late_table", align_bytes=ALIGN)
         word_table = keep.tile([P, T], U32, name="word_table", align_bytes=ALIGN)
         w_raw = keep.tile([P, PACK, N], F32, name="w_raw", tag="raw", align_bytes=ALIGN)
-        w_grouped = keep.tile([P, N, PACK], BF16, name="w_grouped", align_bytes=ALIGN)
+        w_grouped = keep.tile([P, N, PACK], BF16, name="w_grouped", tag="grouped", align_bytes=ALIGN)
         w_codes = keep.tile([P, N], U32, name="w_codes", align_bytes=ALIGN)
         w_bytes = keep.tile([P, N], U8, name="w_bytes", align_bytes=ALIGN)
         picked_bytes = keep.tile([P, S], U8, name="picked_bytes", align_bytes=ALIGN)
@@ -63,8 +64,20 @@ def tile_picked_none_p_kernel(tc, x_words, x_scales, w1, scale, offs, task, out)
             nc.sync.dma_start(x_bytes[r:P:QUADRANT, :].bitcast(I32), picked_bytes[ROW_BASE + r : P : PACK, :].bitcast(I32))
         tables.append(load_table(1, "late_table"))
 
-        x_codes = keep.tile([P, S], U32, name="x_codes", align_bytes=ALIGN)
-        nc.vector.tensor_copy(x_codes[:], word_table[:].indirect(offs_sb[:]))
+        early_codes = keep.tile([P, EARLY], U32, name="early_codes", align_bytes=ALIGN)
+        nc.vector.tensor_copy(early_codes[:], word_table[:].indirect(entries(offs_sb, 0, EARLY)))
+
+        nc.scalar.copy(
+            w_grouped[:, 0:P, :].rearrange("p (c i) j -> p c j i", i=PACK),
+            w_raw[:, :, 0:P].rearrange("p j (c i) -> p c j i", i=PACK),
+        )
+        nc.gpsimd.tensor_scalar(w_grouped[:, P:N, :], w_raw[:, :, P:N].rearrange("p j n -> p n j"), 1.0, 0.0, MULT, ADD)
+        nc.vector.quantize_mx(out=w_codes[:].bitcast(FP8X4), scales=w_bytes[:], in_=w_grouped[:].rearrange("p n j -> p (n j)"))
+        late_codes = keep.tile([P, S - EARLY], U32, name="late_codes", tag="raw", align_bytes=ALIGN)
+        nc.vector.tensor_copy(late_codes[:], word_table[:].indirect(entries(offs_sb, EARLY, S)))
+
+        def x_codes(c, d):
+            return early_codes[:, c:d] if d <= EARLY else late_codes[:, c - EARLY : d - EARLY]
 
         def product(m, *cuts):
             a, b = cuts[0], cuts[-1]
@@ -74,7 +87,7 @@ def tile_picked_none_p_kernel(tc, x_words, x_scales, w1, scale, offs, task, out)
                     out=acc[:, c - a : d - a],
                     lhsT=w_codes[:, m * P : (m + 1) * P].bitcast(FP8X4),
                     lhsT_scale=w_bytes[:, m * P : (m + 1) * P],
-                    rhs=x_codes[:, c:d].bitcast(FP8X4),
+                    rhs=x_codes(c, d).bitcast(FP8X4),
                     rhs_scale=x_bytes[:, c:d],
                     start=True,
                     stop=True,
@@ -98,20 +111,8 @@ def tile_picked_none_p_kernel(tc, x_words, x_scales, w1, scale, offs, task, out)
             queue = nc.scalar if (m, b) == (1, S) else nc.sync
             queue.dma_start(out[m * P : (m + 1) * P, a:b], scaled[:])
 
-        for m in range(N // P):
-            cols = slice(m * P, (m + 1) * P)
-            if m == 0:
-                nc.scalar.copy(
-                    w_grouped[:, cols, :].rearrange("p (c i) j -> p c j i", i=PACK),
-                    w_raw[:, :, cols].rearrange("p j (c i) -> p c j i", i=PACK),
-                )
-            else:
-                nc.gpsimd.tensor_scalar(w_grouped[:, cols, :], w_raw[:, :, cols].rearrange("p j n -> p n j"), 1.0, 0.0, MULT, ADD)
-            nc.vector.quantize_mx(
-                out=w_codes[:, cols].bitcast(FP8X4), scales=w_bytes[:, cols], in_=w_grouped[:, cols, :].rearrange("p n j -> p (n j)")
-            )
         first = look_up(0, 0, 256)
-        second = new_tile("looked0", 256, 640, "raw")
+        second = new_tile("looked0", 256, 640, "grouped")
         nc.vector.tensor_copy(second[:], table_columns(0, 256, 640))
         third = look_up(0, 640, 1024)
         multiply(0, 0, 256, product(0, 0, 256)[:], first)

@@ -22,6 +22,8 @@ QUADRANT = 32
 ROW_BASE = P - K // QUADRANT
 LIST = 16
 ALIGN = 256
+SHARE = 704
+AHEAD = 512
 EARLY = 896
 
 
@@ -46,10 +48,8 @@ def tile_picked_none_p_kernel(tc, x_words, x_scales, w1, scale, offs, task, out)
         def entries(list_tile, a, b):
             return list_tile[:, a // LIST : b // LIST]
 
-        def load_table(m, tag):
-            table = keep.tile([P, U], F32, name=f"scale_table{m}", tag=tag, align_bytes=ALIGN)
-            nc.sync.dma_start(table[:], scale[m * P : (m + 1) * P, :])
-            return table
+        def load_table(m, a, b):
+            nc.sync.dma_start(tables[m][:, a:b], scale[m * P : (m + 1) * P, a:b])
 
         nc.vector.memset(byte_table[0:ROW_BASE, :].bitcast(I32), 0)
         nc.sync.dma_start(offs_sb[:], offs)
@@ -57,12 +57,15 @@ def tile_picked_none_p_kernel(tc, x_words, x_scales, w1, scale, offs, task, out)
         nc.sync.dma_start(word_table[:].bitcast(I32), x_words[0].rearrange("p t r -> p (t r)").bitcast(I32))
         nc.sync.dma_start(w_raw[:], w1.rearrange("(p j) n -> p j n", j=PACK))
         nc.sync.dma_start(task_sb[:], task)
-        tables = [load_table(0, "early_table")]
+        tables = [keep.tile([P, U], F32, name="early_table", align_bytes=ALIGN)]
+        load_table(0, 0, U)
 
         nc.vector.tensor_copy(picked_bytes[:], byte_table[:].indirect(offs_sb[:]))
+        tables.append(keep.tile([P, U], F32, name="late_table", tag="late_table", align_bytes=ALIGN))
+        load_table(1, 0, AHEAD)
         for r in range(PACK):
             nc.sync.dma_start(x_bytes[r:P:QUADRANT, :].bitcast(I32), picked_bytes[ROW_BASE + r : P : PACK, :].bitcast(I32))
-        tables.append(load_table(1, "late_table"))
+        load_table(1, AHEAD, U)
 
         early_codes = keep.tile([P, EARLY], U32, name="early_codes", align_bytes=ALIGN)
         nc.vector.tensor_copy(early_codes[:], word_table[:].indirect(entries(offs_sb, 0, EARLY)))
@@ -105,22 +108,24 @@ def tile_picked_none_p_kernel(tc, x_words, x_scales, w1, scale, offs, task, out)
             nc.scalar.activation(looked[:], table_columns(m, a, b), COPY)
             return looked
 
-        def multiply(m, a, b, first, second):
-            scaled = new_tile(f"scaled{m}", a, b, f"scaled{m}_{a}")
-            nc.vector.tensor_tensor(scaled[:], first, second[:], MULT)
+        def store(m, a, b, scaled):
             queue = nc.scalar if (m, b) == (1, S) else nc.sync
             queue.dma_start(out[m * P : (m + 1) * P, a:b], scaled[:])
 
+        def multiply(m, a, b, first, second):
+            scaled = new_tile(f"scaled{m}", a, b, f"scaled{m}_{a}")
+            nc.vector.tensor_tensor(scaled[:], first, second[:], MULT)
+            store(m, a, b, scaled)
+
         first = look_up(0, 0, 256)
-        second = new_tile("looked0", 256, 640, "grouped")
-        nc.vector.tensor_copy(second[:], table_columns(0, 256, 640))
-        third = look_up(0, 640, 1024)
-        multiply(0, 0, 256, product(0, 0, 256)[:], first)
-        y = new_tile("y", 0, 256, "y")
-        nc.scalar.copy(y[:], product(1, 0, 256)[:])
-        multiply(0, 256, 640, product(0, 256, 512, 640)[:], second)
-        multiply(0, 640, 1024, product(0, 640, 896, 1024)[:], third)
-        multiply(1, 0, 256, table_columns(1, 0, 256), y)
-        for cuts in ((256, 512, 640), (640, 896), (896, 1024)):
+        rest = new_tile("looked0", 256, S, "grouped")
+        nc.vector.tensor_copy(rest[:, 0 : SHARE - 256], table_columns(0, 256, SHARE))
+        nc.scalar.activation(rest[:, SHARE - 256 : S - 256], table_columns(0, SHARE, S), COPY)
+        joined = new_tile("joined", 0, 640, "joined")
+        nc.vector.tensor_tensor(joined[:, 0:256], product(0, 0, 256)[:], first[:], MULT)
+        nc.vector.tensor_tensor(joined[:, 256:640], product(0, 256, 512, 640)[:], rest[:, 0:384], MULT)
+        store(0, 0, 640, joined)
+        multiply(0, 640, 1024, product(0, 640, 896, 1024)[:], rest[:, 384:768])
+        for cuts in ((0, 256, 384), (384, 640), (640, 896), (896, 1024)):
             a, b = cuts[0], cuts[-1]
             multiply(1, a, b, product(1, *cuts)[:], look_up(1, a, b))

@@ -23,7 +23,7 @@ ROW_BASE = P - K // QUADRANT
 LIST = 16
 ALIGN = 256
 SHARE = 704
-AHEAD = 512
+AHEAD = 384
 EARLY = 896
 
 

@@ -22,9 +22,9 @@ QUADRANT = 32
 ROW_BASE = P - K // QUADRANT
 LIST = 16
 ALIGN = 256
+CAST = 192
 SHARE = 704
 AHEAD = 384
-EARLY = 896
 
 
 def tile_picked_none_p_kernel(tc, x_words, x_scales, w1, scale, offs, task, out):
@@ -39,7 +39,7 @@ def tile_picked_none_p_kernel(tc, x_words, x_scales, w1, scale, offs, task, out)
         byte_table = keep.tile([P, T], U8, name="byte_table", tag="late_table", align_bytes=ALIGN)
         word_table = keep.tile([P, T], U32, name="word_table", align_bytes=ALIGN)
         w_raw = keep.tile([P, PACK, N], F32, name="w_raw", tag="raw", align_bytes=ALIGN)
-        w_grouped = keep.tile([P, N, PACK], BF16, name="w_grouped", tag="grouped", align_bytes=ALIGN)
+        w_grouped = keep.tile([P, N, PACK], BF16, name="w_grouped", align_bytes=ALIGN)
         w_codes = keep.tile([P, N], U32, name="w_codes", align_bytes=ALIGN)
         w_bytes = keep.tile([P, N], U8, name="w_bytes", align_bytes=ALIGN)
         picked_bytes = keep.tile([P, S], U8, name="picked_bytes", align_bytes=ALIGN)
@@ -67,20 +67,15 @@ def tile_picked_none_p_kernel(tc, x_words, x_scales, w1, scale, offs, task, out)
             nc.sync.dma_start(x_bytes[r:P:QUADRANT, :].bitcast(I32), picked_bytes[ROW_BASE + r : P : PACK, :].bitcast(I32))
         load_table(1, AHEAD, U)
 
-        early_codes = keep.tile([P, EARLY], U32, name="early_codes", align_bytes=ALIGN)
-        nc.vector.tensor_copy(early_codes[:], word_table[:].indirect(entries(offs_sb, 0, EARLY)))
+        x_codes = keep.tile([P, S], U32, name="x_codes", align_bytes=ALIGN)
+        nc.vector.tensor_copy(x_codes[:], word_table[:].indirect(offs_sb[:]))
 
         nc.scalar.copy(
-            w_grouped[:, 0:P, :].rearrange("p (c i) j -> p c j i", i=PACK),
-            w_raw[:, :, 0:P].rearrange("p j (c i) -> p c j i", i=PACK),
+            w_grouped[:, 0:CAST, :].rearrange("p (c i) j -> p c j i", i=PACK),
+            w_raw[:, :, 0:CAST].rearrange("p j (c i) -> p c j i", i=PACK),
         )
-        nc.gpsimd.tensor_scalar(w_grouped[:, P:N, :], w_raw[:, :, P:N].rearrange("p j n -> p n j"), 1.0, 0.0, MULT, ADD)
+        nc.gpsimd.tensor_scalar(w_grouped[:, CAST:N, :], w_raw[:, :, CAST:N].rearrange("p j n -> p n j"), 1.0, 0.0, MULT, ADD)
         nc.vector.quantize_mx(out=w_codes[:].bitcast(FP8X4), scales=w_bytes[:], in_=w_grouped[:].rearrange("p n j -> p (n j)"))
-        late_codes = keep.tile([P, S - EARLY], U32, name="late_codes", tag="raw", align_bytes=ALIGN)
-        nc.vector.tensor_copy(late_codes[:], word_table[:].indirect(entries(offs_sb, EARLY, S)))
-
-        def x_codes(c, d):
-            return early_codes[:, c:d] if d <= EARLY else late_codes[:, c - EARLY : d - EARLY]
 
         def product(m, *cuts):
             a, b = cuts[0], cuts[-1]
@@ -90,7 +85,7 @@ def tile_picked_none_p_kernel(tc, x_words, x_scales, w1, scale, offs, task, out)
                     out=acc[:, c - a : d - a],
                     lhsT=w_codes[:, m * P : (m + 1) * P].bitcast(FP8X4),
                     lhsT_scale=w_bytes[:, m * P : (m + 1) * P],
-                    rhs=x_codes(c, d).bitcast(FP8X4),
+                    rhs=x_codes[:, c:d].bitcast(FP8X4),
                     rhs_scale=x_bytes[:, c:d],
                     start=True,
                     stop=True,
@@ -118,7 +113,7 @@ def tile_picked_none_p_kernel(tc, x_words, x_scales, w1, scale, offs, task, out)
             store(m, a, b, scaled)
 
         first = look_up(0, 0, 256)
-        rest = new_tile("looked0", 256, S, "grouped")
+        rest = new_tile("looked0", 256, S, "raw")
         nc.vector.tensor_copy(rest[:, 0 : SHARE - 256], table_columns(0, 256, SHARE))
         nc.scalar.activation(rest[:, SHARE - 256 : S - 256], table_columns(0, SHARE, S), COPY)
         joined = new_tile("joined", 0, 640, "joined")

from contextlib import ExitStack

import concourse.mybir as mybir

K, T, S, N, U = 512, 2048, 1024, 256, 1024
FLOPS = 2 * K * N * S

F32 = mybir.dt.float32
BF16 = mybir.dt.bfloat16
I32 = mybir.dt.int32
U32 = mybir.dt.uint32
U16 = mybir.dt.uint16
U8 = mybir.dt.uint8
FP8X4 = mybir.dt.float8_e4m3fn_x4
MULT = mybir.AluOpType.mult
ADD = mybir.AluOpType.add
COPY = mybir.ActivationFunctionType.Copy

P = 128
PACK = 4
QUADRANT = 32
ROW_BASE = P - K // QUADRANT
LIST = 16
ALIGN = 256
CAST = 192
SHARE = 704
AHEAD = 384


def tile_picked_none_p_kernel(tc, x_words, x_scales, w1, scale, offs, task, out):
    nc = tc.nc
    with ExitStack() as ctx:
        lists = ctx.enter_context(tc.tile_pool(name="lists", bufs=1))
        keep = ctx.enter_context(tc.tile_pool(name="keep", bufs=1))
        psum = ctx.enter_context(tc.psum_pool(name="psum", bufs=1))

        offs_sb = lists.tile([P, S // LIST], U16, name="offs_sb")
        task_sb = lists.tile([P, S // LIST], U16, name="task_sb")
        byte_table = keep.tile([P, T], U8, name="byte_table", tag="late_table", align_bytes=ALIGN)
        word_table = keep.tile([P, T], U32, name="word_table", align_bytes=ALIGN)
        w_raw = keep.tile([P, PACK, N], F32, name="w_raw", tag="raw", align_bytes=ALIGN)
        w_grouped = keep.tile([P, N, PACK], BF16, name="w_grouped", align_bytes=ALIGN)
        w_codes = keep.tile([P, N], U32, name="w_codes", align_bytes=ALIGN)
        w_bytes = keep.tile([P, N], U8, name="w_bytes", align_bytes=ALIGN)
        picked_bytes = keep.tile([P, S], U8, name="picked_bytes", align_bytes=ALIGN)
        x_bytes = keep.tile([P, S], U8, name="x_bytes", align_bytes=ALIGN)

        def entries(list_tile, a, b):
            return list_tile[:, a // LIST : b // LIST]

        def load_table(m, a, b):
            nc.sync.dma_start(tables[m][:, a:b], scale[m * P : (m + 1) * P, a:b])

        nc.vector.memset(byte_table[0:ROW_BASE, :].bitcast(I32), 0)
        nc.sync.dma_start(offs_sb[:], offs)
        nc.scalar.dma_start(byte_table[ROW_BASE:P, :].bitcast(I32), x_scales[0].bitcast(I32))
        nc.sync.dma_start(word_table[:].bitcast(I32), x_words[0].rearrange("p t r -> p (t r)").bitcast(I32))
        nc.sync.dma_start(w_raw[:], w1.rearrange("(p j) n -> p j n", j=PACK))
        nc.sync.dma_start(task_sb[:], task)
        tables = [keep.tile([P, U], F32, name="early_table", align_bytes=ALIGN)]
        load_table(0, 0, U)

        nc.vector.tensor_copy(picked_bytes[:], byte_table[:].indirect(offs_sb[:]))
        tables.append(keep.tile([P, U], F32, name="late_table", tag="late_table", align_bytes=ALIGN))
        load_table(1, 0, AHEAD)
        for r in range(PACK):
            nc.sync.dma_start(x_bytes[r:P:QUADRANT, :].bitcast(I32), picked_bytes[ROW_BASE + r : P : PACK, :].bitcast(I32))
        load_table(1, AHEAD, U)

        x_codes = keep.tile([P, S], U32, name="x_codes", align_bytes=ALIGN)
        nc.vector.tensor_copy(x_codes[:], word_table[:].indirect(offs_sb[:]))

        nc.scalar.copy(
            w_grouped[:, 0:CAST, :].rearrange("p (c i) j -> p c j i", i=PACK),
            w_raw[:, :, 0:CAST].rearrange("p j (c i) -> p c j i", i=PACK),
        )
        nc.gpsimd.tensor_scalar(w_grouped[:, CAST:N, :], w_raw[:, :, CAST:N].rearrange("p j n -> p n j"), 1.0, 0.0, MULT, ADD)
        nc.vector.quantize_mx(out=w_codes[:].bitcast(FP8X4), scales=w_bytes[:], in_=w_grouped[:].rearrange("p n j -> p (n j)"))

        def product(m, *cuts):
            a, b = cuts[0], cuts[-1]
            acc = psum.tile([P, b - a], F32, name=f"acc{m}_{a}")
            for c, d in zip(cuts, cuts[1:]):
                nc.tensor.matmul_mx(
                    out=acc[:, c - a : d - a],
                    lhsT=w_codes[:, m * P : (m + 1) * P].bitcast(FP8X4),
                    lhsT_scale=w_bytes[:, m * P : (m + 1) * P],
                    rhs=x_codes[:, c:d].bitcast(FP8X4),
                    rhs_scale=x_bytes[:, c:d],
                    start=True,
                    stop=True,
                )
            return acc

        def new_tile(name, a, b, tag):
            return keep.tile([P, b - a], F32, name=f"{name}_{a}", tag=tag, align_bytes=ALIGN)

        def table_columns(m, a, b):
            return tables[m][:].indirect(entries(task_sb, a, b))

        def look_up(m, a, b):
            looked = new_tile(f"looked{m}", a, b, f"looked{m}_{a}")
            nc.scalar.activation(looked[:], table_columns(m, a, b), COPY)
            return looked

        def store(m, a, b, scaled):
            queue = nc.scalar if (m, b) == (1, S) else nc.sync
            queue.dma_start(out[m * P : (m + 1) * P, a:b], scaled[:])

        def multiply(m, a, b, first, second):
            scaled = new_tile(f"scaled{m}", a, b, f"scaled{m}_{a}")
            nc.vector.tensor_tensor(scaled[:], first, second[:], MULT)
            store(m, a, b, scaled)

        first = look_up(0, 0, 256)
        rest = new_tile("looked0", 256, S, "raw")
        nc.vector.tensor_copy(rest[:, 0 : SHARE - 256], table_columns(0, 256, SHARE))
        nc.scalar.activation(rest[:, SHARE - 256 : S - 256], table_columns(0, SHARE, S), COPY)
        joined = new_tile("joined", 0, 640, "joined")
        nc.vector.tensor_tensor(joined[:, 0:256], product(0, 0, 256)[:], first[:], MULT)
        nc.vector.tensor_tensor(joined[:, 256:640], product(0, 256, 512, 640)[:], rest[:, 0:384], MULT)
        store(0, 0, 640, joined)
        multiply(0, 640, 1024, product(0, 640, 896, 1024)[:], rest[:, 384:768])
        for cuts in ((0, 256, 384), (384, 640), (640, 896), (896, 1024)):
            a, b = cuts[0], cuts[-1]
            multiply(1, a, b, product(1, *cuts)[:], look_up(1, a, b))
